import numpy as np
import ml_dtypes


def mxq(x, axis, fmt="e4m3"):
    dtype, down = {"e4m3": (ml_dtypes.float8_e4m3fn, 7), "e5m2": (ml_dtypes.float8_e5m2, 14)}[fmt]
    v = np.moveaxis(np.asarray(x, np.float32).astype(ml_dtypes.bfloat16).astype(np.float64), axis, -1)
    blocks = v.reshape(v.shape[:-1] + (-1, 32))
    amax = np.abs(blocks).max(-1, keepdims=True)
    byte = np.maximum(np.where(amax > 0, np.frexp(amax)[1] - 1 + 127, 0) - down, 1)
    scale = np.exp2(byte - 127.0)
    codes = (blocks / scale).astype(np.float32).astype(dtype).astype(np.float64)
    return np.moveaxis((codes * scale).reshape(v.shape), -1, axis)


WIDE = False


def mx_kscale(k):
    if not WIDE:
        return np.ones(k)
    levels = np.array([10, -10, 5, -5, 0])
    if k % 512:
        return np.exp2(np.random.permutation(np.resize(levels, k // 32))).repeat(32)
    a = np.empty((k // 512, 16))
    for p in range(k // 512):
        a[p, :8] = np.random.permutation(np.resize(levels, 8))
        for g in range(8):
            far = levels[np.abs(levels - a[p, g]) >= 10]
            a[p, g + 8] = far[np.random.randint(len(far))]
    return np.exp2(a.ravel()).repeat(32)


def f64(x):
    return np.asarray(x).astype(np.float64)


def striped(idx):
    return np.tile(np.asarray(idx).reshape(-1, 16).T, (8, 1)).astype(np.uint16)


def unstriped(offs):
    return offs[:16].T.reshape(-1).astype(np.int64)


E2M1 = np.array([0.0, 0.5, 1.0, 1.5, 2.0, 3.0, 4.0, 6.0, -0.0, -0.5, -1.0, -1.5, -2.0, -3.0, -4.0, -6.0])


def pack_weight(w, fmt):
    k, n = w.shape
    w = f64(np.asarray(w, np.float32).astype(ml_dtypes.bfloat16)).reshape(k // 32, 32, n)
    amax = np.abs(w).max(1)
    if fmt == "e4m3":
        byte = np.frexp(amax)[1] - 1 + 127 - 7
    else:
        mant, ex = np.frexp(amax / 6.0)
        byte = np.where(mant > 0.5, ex, ex - 1) + 127
    byte = np.clip(np.where(amax > 0, byte, 1), 1, 254)
    scaled = (w * np.exp2(127.0 - byte)[:, None, :]).reshape(k, n).astype(np.float32)
    by_word = np.ascontiguousarray(scaled.reshape(k // 512, 128, 4, n).transpose(0, 1, 3, 2))
    if fmt == "e4m3":
        words = by_word.astype(ml_dtypes.float8_e4m3fn).view(np.uint8)
    else:
        c = by_word.astype(ml_dtypes.float4_e2m1fn).view(np.uint8) & 0xF
        words = (c[..., 0::2] | (c[..., 1::2] << 4)).reshape(k // 512, 128, 2 * n)
    return np.ascontiguousarray(words), np.ascontiguousarray(byte.astype(np.uint8).reshape(k // 512, 16, n))


def unpack_weight(words, scales, fmt):
    g, _, n = scales.shape
    words = np.ascontiguousarray(words).reshape(g, 128, n, -1)
    if fmt == "e4m3":
        vals = words.view(ml_dtypes.float8_e4m3fn).astype(np.float64)
    else:
        nib = np.empty((g, 128, n, 4), np.uint8)
        nib[..., 0::2] = words & 0xF
        nib[..., 1::2] = words >> 4
        vals = E2M1[nib]
    vals = vals * np.repeat(np.exp2(scales.astype(np.float64) - 127.0), 8, axis=1)[..., None]
    return vals.transpose(0, 1, 3, 2).reshape(g * 512, n)


B, N, T, D, DV, NQ = 1, 1536, 4096, 1024, 256, 256
PAGE = 512


def setup_inputs():
    n = np.random.standard_normal
    pages = np.random.permutation(T // PAGE)[:B * N // PAGE]
    idx = (pages[:, None] * PAGE + np.arange(PAGE)[None, :]).reshape(-1)
    s = mx_kscale(D)[:, None]
    u = np.ones(T)
    u[idx] = mx_kscale(B * N)
    r = np.random.uniform(0.5, 2.0, T)
    qp = [pack_weight(x, "e4m3") for x in n((B, D, NQ)) * s * (1.00 / np.sqrt(D))]
    k = n((D, T)) / s
    v = n((DV, T)) / (u * r)
    kp = pack_weight(k, "e2m1")
    vp = pack_weight(v.T, "e4m3")
    return {
        "q_words": np.stack([x[0] for x in qp]),
        "q_scales": np.stack([x[1] for x in qp]),
        "k_words": np.ascontiguousarray(kp[0].reshape(D // 1024, 2, 128, T, 2).transpose(0, 2, 3, 1, 4)).reshape(D // 1024, 128, T, 4),
        "k_scales": kp[1],
        "v_words": vp[0],
        "v_scales": vp[1],
        "vs": np.tile(u * r, (128, 1)).astype(np.float32),
        "kb": np.tile(n(T), (128, 1)).astype(np.float32),
        "offs": striped(idx),
        "voffs": striped((pages[:, None] * DV + np.arange(DV)[None, :]).reshape(-1)),
    }


def reference(q_words, q_scales, k_words, k_scales, v_words, v_scales, vs, kb, offs, voffs):
    idx = unstriped(offs)
    k = unpack_weight(k_words.reshape(D // 1024, 128, T, 2, 2).transpose(0, 3, 1, 2, 4).reshape(D // 512, 128, 2 * T), k_scales, "e2m1")
    v = unpack_weight(v_words, v_scales, "e4m3")
    v = v.reshape(T // 512, 512, DV)[unstriped(voffs)[::DV] // DV].reshape(B, N, DV)
    pick = lambda x: x[:, idx].reshape(x.shape[0], B, N).transpose(1, 0, 2)
    q = np.stack([unpack_weight(q_words[b], q_scales[b], "e4m3") for b in range(B)])
    score = q.transpose(0, 2, 1) @ pick(k)
    score = score + pick(f64(kb))[:, :1, :]
    m = score.max(-1, keepdims=True)
    p = np.exp(score - m)
    total = p.sum(-1, keepdims=True)
    w = p * pick(f64(vs))[:, :1, :]
    y = mxq(w, 2, "e4m3") @ v
    y = y / total
    return y

@@ -1,0 +1,259 @@
+from contextlib import ExitStack
+
+import concourse.mybir as mybir
+from concourse.masks import make_identity
+
+N, T, D, DV, NQ = 1536, 4096, 1024, 256, 256
+PAGE = 512
+FLOPS = 2 * NQ * N * (D + DV)
+
+F32 = mybir.dt.float32
+BF16 = mybir.dt.bfloat16
+I32 = mybir.dt.int32
+U32 = mybir.dt.uint32
+U16 = mybir.dt.uint16
+U8 = mybir.dt.uint8
+FP8X4 = mybir.dt.float8_e4m3fn_x4
+FP4X4 = mybir.dt.float4_e2m1fn_x4
+ACT = mybir.ActivationFunctionType
+ALU = mybir.AluOpType
+AXIS = mybir.AxisListType
+
+P = 128
+PACK = 4
+PAGES = N // PAGE
+POOL_PAGES = T // PAGE
+PASSES = D // (P * PACK)
+HALVES = NQ // P
+TILES = PAGE // P
+QUADS = 4
+LIST_ROW = 16
+
+
+def tile_attend_pkv4q_soft_kb_kernel(
+    tc, q_words, q_scales, k_words, k_scales, v_words, v_scales, vs, kb, offs, voffs, out
+):
+    nc = tc.nc
+    with ExitStack() as ctx:
+        keep = ctx.enter_context(tc.tile_pool(name="keep", bufs=1))
+        psum = ctx.enter_context(tc.psum_pool(name="psum", bufs=1))
+
+        def sbuf(name, shape, dtype, tag=""):
+            return keep.tile(shape, dtype, name=name, tag=tag, align_bytes=64)
+
+        def bank(index, name):
+            return psum.tile([P, PAGE], F32, name=name, tag="bank%d" % index)
+
+        offsets = keep.tile([P, N // LIST_ROW], U16, name="offsets")
+        voffsets = keep.tile([P, PAGES * DV // LIST_ROW], U16, name="voffsets")
+        kw_pool = sbuf("kw_pool", [P, T], U32)
+        ks_pool = sbuf("ks_pool", [P, T], U8, "first")
+        vsc_pool = sbuf("vsc_pool", [P, POOL_PAGES * DV], U8, "second")
+        kb_pool = sbuf("kb_pool", [P, T], F32)
+        qw = sbuf("qw", [P, PASSES * NQ], U32)
+        qs = sbuf("qs", [P, PASSES * NQ], U8)
+        k_planes = sbuf("k_planes", [P, PASSES * N], U8)
+        ident = sbuf("ident", [P, P], F32)
+        warm = sbuf("warm", [P, 2], F32)
+
+        nc.vector.memset(ks_pool[32:64, :].bitcast(I32), 0)
+        nc.vector.memset(ks_pool[64:128, :].bitcast(I32), 0)
+        nc.gpsimd.memset(vsc_pool[:].bitcast(I32), 0)
+        nc.gpsimd.memset(qs[:].bitcast(I32), 0)
+        make_identity(nc, ident[:])
+        nc.gpsimd.memset(k_planes[:].bitcast(I32), 0)
+        nc.gpsimd.memset(kb_pool[:], 0.0)
+        nc.scalar.activation(out=warm[:], in_=ident[:, 0:2], func=ACT.Exp)
+
+        nc.sync.dma_start(offsets[:], offs)
+        nc.sync.dma_start(ks_pool[0:32, :].bitcast(I32), k_scales.rearrange("o f t -> f o t").bitcast(I32))
+        nc.sync.dma_start(kw_pool[:].bitcast(I32), k_words[0].rearrange("p t b -> p (t b)").bitcast(I32))
+        nc.sync.dma_start(voffsets[:], voffs)
+        for quad in range(QUADS):
+            nc.sync.dma_start(
+                vsc_pool[32 * quad : 32 * quad + 4, :].bitcast(I32).rearrange("f (u e) -> f u e", u=POOL_PAGES),
+                v_scales[:, 4 * quad : 4 * quad + 4, :].rearrange("u f e -> f u e").bitcast(I32),
+            )
+        nc.sync.dma_start(
+            qw[:].bitcast(I32).rearrange("p (o q) -> p o q", o=PASSES),
+            q_words[0].rearrange("o p q r -> p o (q r)").bitcast(I32),
+        )
+        for quad in range(QUADS):
+            nc.sync.dma_start(
+                qs[32 * quad : 32 * quad + 4, :].bitcast(I32).rearrange("f (o q) -> f o q", o=PASSES),
+                q_scales[0, :, 4 * quad : 4 * quad + 4, :].rearrange("o f q -> f o q").bitcast(I32),
+            )
+
+        ks_rows = sbuf("ks_rows", [P, N], U8)
+        nc.vector.tensor_copy(ks_rows[:], ks_pool[:].indirect(offsets[:]))
+        for quad in range(QUADS):
+            nc.sync.dma_start(
+                k_planes[32 * quad : 32 * quad + 4, :].bitcast(I32).rearrange("f (o n) -> f o n", o=PASSES),
+                ks_rows[8 * quad : 8 * quad + 8, :].bitcast(I32),
+            )
+        nc.sync.dma_start(kb_pool[0:1, :], kb[0:1, :])
+        vs_pool = sbuf("vs_pool", [P, T], F32, "first")
+        nc.sync.dma_start(vs_pool[:], vs)
+
+        vsc = sbuf("vsc", [P, PAGES * DV], U8)
+        nc.vector.tensor_copy(vsc[:], vsc_pool[:].indirect(voffsets[:]))
+        vw_pool = sbuf("vw_pool", [P, POOL_PAGES * DV], U32, "second")
+        nc.sync.dma_start(
+            vw_pool[:].bitcast(I32).rearrange("p (u e) -> p u e", u=POOL_PAGES),
+            v_words.rearrange("u p e r -> p u (e r)").bitcast(I32),
+        )
+
+        def page_offsets(e):
+            cols = PAGE // LIST_ROW
+            return offsets[:, e * cols : (e + 1) * cols]
+
+        def bias_columns(e):
+            row = sbuf("kb_row%d" % e, [P, PAGE], F32)
+            nc.vector.tensor_copy(row[:], kb_pool[:].indirect(page_offsets(e)))
+            turned = bank((0, 1, 3)[e], "kb_turned%d" % e)
+            for j in range(TILES):
+                nc.tensor.transpose(turned[:, j * P : (j + 1) * P], row[:, j * P : (j + 1) * P], ident[:])
+            cols = sbuf("kb_cols%d" % e, [P, TILES], F32)
+            nc.scalar.copy(cols[:], turned[:, 0:PAGE:P])
+            return cols
+
+        scores = [[None] * PAGES for h in range(HALVES)]
+        page_max = [sbuf("page_max%d" % h, [P, PAGES], F32) for h in range(HALVES)]
+
+        def gather_keys(e):
+            pairs = sbuf("k_pairs%d" % e, [P, PAGE], U32)
+            nc.vector.tensor_copy(pairs[:], kw_pool[:].indirect(page_offsets(e)))
+            words = sbuf("k_parted%d" % e, [P, PASSES, PAGE], U16)
+            nc.vector.tensor_copy(words[:], pairs[:].bitcast(U16).rearrange("p (n o) -> p o n", o=PASSES))
+            return words
+
+        def raw_scores(e, words):
+            raws = []
+            for pair in range(TILES // 2):
+                raw = bank(((6, 7), (2, 5), (6, 7))[e][pair], "raw%d_%d" % (e, pair))
+                raws.append(raw)
+                for jj in range(2):
+                    j = 2 * pair + jj
+                    for h in range(HALVES):
+                        for o in range(PASSES):
+                            queries = slice(o * NQ + h * P, o * NQ + (h + 1) * P)
+                            lo = o * N + e * PAGE + j * P
+                            nc.tensor.matmul_mx(
+                                out=raw[:, jj * NQ + h * P : jj * NQ + (h + 1) * P],
+                                lhsT=words[:, o, j * P : (j + 1) * P].bitcast(FP4X4),
+                                lhsT_scale=k_planes[:, lo : lo + P],
+                                rhs=qw[:, queries].bitcast(FP8X4),
+                                rhs_scale=qs[:, queries],
+                                start=(o == 0),
+                                stop=(o == PASSES - 1),
+                            )
+            return raws
+
+        def biased_scores(e, raws, kb_cols):
+            for h in range(HALVES):
+                scores[h][e] = bank(h * PAGES + e, "score%d_%d" % (h, e))
+            for j in range(TILES):
+                biased = sbuf("biased%d_%d" % (e, j), [P, NQ], F32)
+                nc.scalar.activation(
+                    out=biased[:],
+                    in_=raws[j // 2][:, (j % 2) * NQ : (j % 2 + 1) * NQ],
+                    func=ACT.Identity,
+                    bias=kb_cols[:, j : j + 1],
+                )
+                for h in range(HALVES):
+                    nc.tensor.transpose(scores[h][e][:, j * P : (j + 1) * P], biased[:, h * P : (h + 1) * P], ident[:])
+
+        def max_page(h, e):
+            nc.vector.tensor_reduce(out=page_max[h][:, e : e + 1], in_=scores[h][e][:], axis=AXIS.X, op=ALU.max)
+
+        keys = [gather_keys(e) for e in range(PAGES)]
+        raws0 = raw_scores(0, keys[0])
+        raws1 = raw_scores(1, keys[1])
+        kb_cols = [bias_columns(e) for e in range(PAGES)]
+        biased_scores(0, raws0, kb_cols[0])
+        raws2 = raw_scores(2, keys[2])
+        biased_scores(1, raws1, kb_cols[1])
+        biased_scores(2, raws2, kb_cols[2])
+
+        vs_row = sbuf("vs_row", [P, N], F32)
+        nc.vector.tensor_copy(vs_row[:], vs_pool[:].indirect(offsets[:]))
+        vs_cols = []
+        for e in range(PAGES):
+            cols = sbuf("vs_cols%d" % e, [P, PACK], F32)
+            nc.sync.dma_start(cols[:], vs_row[0:1, e * PAGE : (e + 1) * PAGE])
+            vs_cols.append(cols)
+
+        for e in range(PAGES - 1):
+            for h in range(HALVES):
+                max_page(h, e)
+
+        vw = sbuf("vw", [P, PAGES * DV], U32)
+        nc.vector.tensor_copy(vw[:], vw_pool[:].indirect(voffsets[:]))
+
+        neg_max = []
+        for h in range(HALVES):
+            max_page(h, PAGES - 1)
+            neg = sbuf("neg_max%d" % h, [P, 1], F32)
+            nc.vector.tensor_reduce(out=neg[:], in_=page_max[h][:], axis=AXIS.X, op=ALU.max, negate=True)
+            neg_max.append(neg)
+
+        page_sum = [sbuf("page_sum%d" % h, [P, PAGES], F32) for h in range(HALVES)]
+        sums = [bank(6 + h, "sums%d" % h) for h in range(HALVES)]
+
+        def weigh(h, e):
+            probs = sbuf("probs%d_%d" % (h, e), [P, PACK, P], F32)
+            nc.scalar.activation(
+                out=probs[:],
+                in_=scores[h][e][:].rearrange("q (s r) -> q r s", r=PACK),
+                func=ACT.Exp,
+                bias=neg_max[h][:],
+                accum_out=page_sum[h][:, e : e + 1],
+            )
+            turned = bank(h * PAGES + e, "probs_turned%d_%d" % (h, e))
+            for r in range(PACK):
+                nc.tensor.transpose(turned[:, r * P : (r + 1) * P], probs[:, r, :], ident[:])
+            weights = sbuf("weights%d_%d" % (h, e), [P, P, PACK], BF16)
+            nc.vector.tensor_tensor(
+                out=weights[:],
+                in0=turned[:].rearrange("s (r q) -> s q r", r=PACK),
+                in1=vs_cols[e][:].unsqueeze(1).to_broadcast([P, P, PACK]),
+                op=ALU.mult,
+            )
+            return weights
+
+        def multiply(h, e, weights):
+            codes = sbuf("w_codes%d_%d" % (h, e), [P, P], U32)
+            plane = sbuf("w_plane%d_%d" % (h, e), [P, P], U8)
+            nc.vector.quantize_mx(
+                out=codes[:].bitcast(FP8X4), scales=plane[:], in_=weights[:].rearrange("s q r -> s (q r)")
+            )
+            nc.tensor.matmul_mx(
+                out=sums[h][:, 0:DV],
+                lhsT=codes[:].bitcast(FP8X4),
+                lhsT_scale=plane[:],
+                rhs=vw[:, e * DV : (e + 1) * DV].bitcast(FP8X4),
+                rhs_scale=vsc[:, e * DV : (e + 1) * DV],
+                start=(e == 0),
+                stop=(e == PAGES - 1),
+            )
+
+        def finish(h):
+            total = sbuf("total%d" % h, [P, 1], F32)
+            nc.vector.tensor_reduce(out=total[:], in_=page_sum[h][:], axis=AXIS.X, op=ALU.add)
+            inverse = sbuf("inverse%d" % h, [P, 1], F32)
+            nc.vector.reciprocal(inverse[:], total[:])
+            result = sbuf("result%d" % h, [P, DV], F32)
+            nc.scalar.activation(out=result[:], in_=sums[h][:, 0:DV], func=ACT.Copy, scale=inverse[:])
+            nc.sync.dma_start(out[0, h * P : (h + 1) * P, :], result[:])
+
+        steps = [(h, e) for h in range(HALVES) for e in range(PAGES)]
+        pending = None
+        for h, e in steps:
+            weights = weigh(h, e)
+            if pending is not None:
+                multiply(*pending)
+                if pending[1] == PAGES - 1:
+                    finish(pending[0])
+            pending = (h, e, weights)
+        multiply(*pending)
+        finish(pending[0])

@@ -46,37 +46,32 @@ def tile_attend_pkv4q_soft_kb_kernel(
 
         offsets = keep.tile([P, N // LIST_ROW], U16, name="offsets")
         voffsets = keep.tile([P, PAGES * DV // LIST_ROW], U16, name="voffsets")
-        kw_pool = sbuf("kw_pool", [P, T], U32)
-        ks_pool = sbuf("ks_pool", [P, T], U8, "first")
-        vsc_pool = sbuf("vsc_pool", [P, POOL_PAGES * DV], U8, "second")
+        kw_pool = sbuf("kw_pool", [P, T], U32, "keys_then_values")
+        ks_pool = sbuf("ks_pool", [P, T], U8)
+        vsc_pool = sbuf("vsc_pool", [P, POOL_PAGES * DV], U8)
         kb_pool = sbuf("kb_pool", [P, T], F32)
-        qw = sbuf("qw", [P, PASSES * NQ], U32)
         qs = sbuf("qs", [P, PASSES * NQ], U8)
         k_planes = sbuf("k_planes", [P, PASSES * N], U8)
-        ident = sbuf("ident", [P, P], F32)
-        warm = sbuf("warm", [P, 2], F32)
 
         nc.vector.memset(ks_pool[32:64, :].bitcast(I32), 0)
         nc.vector.memset(ks_pool[64:128, :].bitcast(I32), 0)
         nc.gpsimd.memset(vsc_pool[:].bitcast(I32), 0)
-        nc.gpsimd.memset(qs[:].bitcast(I32), 0)
-        make_identity(nc, ident[:])
         nc.gpsimd.memset(k_planes[:].bitcast(I32), 0)
+        nc.gpsimd.memset(qs[:].bitcast(I32), 0)
         nc.gpsimd.memset(kb_pool[:], 0.0)
-        nc.scalar.activation(out=warm[:], in_=ident[:, 0:2], func=ACT.Exp)
 
-        nc.sync.dma_start(offsets[:], offs)
         nc.sync.dma_start(ks_pool[0:32, :].bitcast(I32), k_scales.rearrange("o f t -> f o t").bitcast(I32))
+        nc.sync.dma_start(offsets[:], offs)
         nc.sync.dma_start(kw_pool[:].bitcast(I32), k_words[0].rearrange("p t b -> p (t b)").bitcast(I32))
         nc.sync.dma_start(voffsets[:], voffs)
-        for quad in range(QUADS):
-            nc.sync.dma_start(
-                vsc_pool[32 * quad : 32 * quad + 4, :].bitcast(I32).rearrange("f (u e) -> f u e", u=POOL_PAGES),
-                v_scales[:, 4 * quad : 4 * quad + 4, :].rearrange("u f e -> f u e").bitcast(I32),
-            )
+        qw = sbuf("qw", [P, PASSES * NQ], U32)
         nc.sync.dma_start(
             qw[:].bitcast(I32).rearrange("p (o q) -> p o q", o=PASSES),
             q_words[0].rearrange("o p q r -> p o (q r)").bitcast(I32),
+        )
+        nc.sync.dma_start(
+            vsc_pool[0:16, :].bitcast(I32).rearrange("f (u e) -> f u e", u=POOL_PAGES),
+            v_scales.rearrange("u f e -> f u e").bitcast(I32),
         )
         for quad in range(QUADS):
             nc.sync.dma_start(
@@ -91,17 +86,16 @@ def tile_attend_pkv4q_soft_kb_kernel(
                 k_planes[32 * quad : 32 * quad + 4, :].bitcast(I32).rearrange("f (o n) -> f o n", o=PASSES),
                 ks_rows[8 * quad : 8 * quad + 8, :].bitcast(I32),
             )
-        nc.sync.dma_start(kb_pool[0:1, :], kb[0:1, :])
-        vs_pool = sbuf("vs_pool", [P, T], F32, "first")
-        nc.sync.dma_start(vs_pool[:], vs)
+        nc.scalar.dma_start(kb_pool[0:1, :], kb[0:1, :])
 
+        vsc_rows = sbuf("vsc_rows", [P, PAGES * DV], U8)
+        nc.vector.tensor_copy(vsc_rows[:], vsc_pool[:].indirect(voffsets[:]))
         vsc = sbuf("vsc", [P, PAGES * DV], U8)
-        nc.vector.tensor_copy(vsc[:], vsc_pool[:].indirect(voffsets[:]))
-        vw_pool = sbuf("vw_pool", [P, POOL_PAGES * DV], U32, "second")
-        nc.sync.dma_start(
-            vw_pool[:].bitcast(I32).rearrange("p (u e) -> p u e", u=POOL_PAGES),
-            v_words.rearrange("u p e r -> p u (e r)").bitcast(I32),
-        )
+        nc.gpsimd.memset(vsc[:].bitcast(I32), 0)
+        for quad in range(QUADS):
+            nc.sync.dma_start(
+                vsc[32 * quad : 32 * quad + 4, :].bitcast(I32), vsc_rows[4 * quad : 4 * quad + 4, :].bitcast(I32)
+            )
 
         def page_offsets(e):
             cols = PAGE // LIST_ROW
@@ -110,7 +104,7 @@ def tile_attend_pkv4q_soft_kb_kernel(
         def bias_columns(e):
             row = sbuf("kb_row%d" % e, [P, PAGE], F32)
             nc.vector.tensor_copy(row[:], kb_pool[:].indirect(page_offsets(e)))
-            turned = bank((0, 1, 3)[e], "kb_turned%d" % e)
+            turned = bank((0, 1, 0)[e], "kb_turned%d" % e)
             for j in range(TILES):
                 nc.tensor.transpose(turned[:, j * P : (j + 1) * P], row[:, j * P : (j + 1) * P], ident[:])
             cols = sbuf("kb_cols%d" % e, [P, TILES], F32)
@@ -118,19 +112,20 @@ def tile_attend_pkv4q_soft_kb_kernel(
             return cols
 
         scores = [[None] * PAGES for h in range(HALVES)]
-        page_max = [sbuf("page_max%d" % h, [P, PAGES], F32) for h in range(HALVES)]
+        negated = [[None] * PAGES for h in range(HALVES)]
+        neg_max = [None] * HALVES
 
         def gather_keys(e):
-            pairs = sbuf("k_pairs%d" % e, [P, PAGE], U32)
+            pairs = sbuf("k_pairs%d" % e, [P, PAGE], U32, "pairs%d" % e)
             nc.vector.tensor_copy(pairs[:], kw_pool[:].indirect(page_offsets(e)))
-            words = sbuf("k_parted%d" % e, [P, PASSES, PAGE], U16)
+            words = sbuf("k_parted%d" % e, [P, PASSES, PAGE], U16, "parted%d" % e)
             nc.vector.tensor_copy(words[:], pairs[:].bitcast(U16).rearrange("p (n o) -> p o n", o=PASSES))
             return words
 
         def raw_scores(e, words):
             raws = []
             for pair in range(TILES // 2):
-                raw = bank(((6, 7), (2, 5), (6, 7))[e][pair], "raw%d_%d" % (e, pair))
+                raw = bank(2 + 2 * e + pair, "raw%d_%d" % (e, pair))
                 raws.append(raw)
                 for jj in range(2):
                     j = 2 * pair + jj
@@ -151,7 +146,7 @@ def tile_attend_pkv4q_soft_kb_kernel(
 
         def biased_scores(e, raws, kb_cols):
             for h in range(HALVES):
-                scores[h][e] = bank(h * PAGES + e, "score%d_%d" % (h, e))
+                scores[h][e] = bank(2 * e + h, "score%d_%d" % (h, e))
             for j in range(TILES):
                 biased = sbuf("biased%d_%d" % (e, j), [P, NQ], F32)
                 nc.scalar.activation(
@@ -164,16 +159,33 @@ def tile_attend_pkv4q_soft_kb_kernel(
                     nc.tensor.transpose(scores[h][e][:, j * P : (j + 1) * P], biased[:, h * P : (h + 1) * P], ident[:])
 
         def max_page(h, e):
-            nc.vector.tensor_reduce(out=page_max[h][:, e : e + 1], in_=scores[h][e][:], axis=AXIS.X, op=ALU.max)
+            negated[h][e] = sbuf("negated%d_%d" % (h, e), [P, PACK, P], F32)
+            least = sbuf("neg_max%d_%d" % (h, e), [P, 1], F32, "neg_max%d_%d" % (h, e))
+            nc.vector.tensor_scalar(
+                out=negated[h][e][:],
+                in0=scores[h][e][:].rearrange("q (s r) -> q r s", r=PACK),
+                scalar1=-1.0,
+                scalar2=neg_max[h][:] if e > 0 else None,
+                op0=ALU.mult,
+                op1=ALU.min,
+                accum_out=least[:],
+            )
+            neg_max[h] = least
 
-        keys = [gather_keys(e) for e in range(PAGES)]
-        raws0 = raw_scores(0, keys[0])
-        raws1 = raw_scores(1, keys[1])
+        raws = [raw_scores(e, gather_keys(e)) for e in range(PAGES)]
+        ident = sbuf("ident", [P, P], F32, "parted0")
+        make_identity(nc, ident[:])
         kb_cols = [bias_columns(e) for e in range(PAGES)]
-        biased_scores(0, raws0, kb_cols[0])
-        raws2 = raw_scores(2, keys[2])
-        biased_scores(1, raws1, kb_cols[1])
-        biased_scores(2, raws2, kb_cols[2])
+        for e in range(PAGES):
+            biased_scores(e, raws[e], kb_cols[e])
+
+        vs_pool = sbuf("vs_pool", [P, T], F32, "pairs0")
+        nc.scalar.dma_start(vs_pool[:], vs)
+        vw_pool = sbuf("vw_pool", [P, POOL_PAGES * DV], U32, "keys_then_values")
+        nc.scalar.dma_start(
+            vw_pool[:].bitcast(I32).rearrange("p (u e) -> p u e", u=POOL_PAGES),
+            v_words.rearrange("u p e r -> p u (e r)").bitcast(I32),
+        )
 
         vs_row = sbuf("vs_row", [P, N], F32)
         nc.vector.tensor_copy(vs_row[:], vs_pool[:].indirect(offsets[:]))
@@ -183,19 +195,12 @@ def tile_attend_pkv4q_soft_kb_kernel(
             nc.sync.dma_start(cols[:], vs_row[0:1, e * PAGE : (e + 1) * PAGE])
             vs_cols.append(cols)
 
-        for e in range(PAGES - 1):
+        for e in range(PAGES):
             for h in range(HALVES):
                 max_page(h, e)
 
-        vw = sbuf("vw", [P, PAGES * DV], U32)
+        vw = sbuf("vw", [P, PAGES * DV], U32, "neg_max0_1")
         nc.vector.tensor_copy(vw[:], vw_pool[:].indirect(voffsets[:]))
-
-        neg_max = []
-        for h in range(HALVES):
-            max_page(h, PAGES - 1)
-            neg = sbuf("neg_max%d" % h, [P, 1], F32)
-            nc.vector.tensor_reduce(out=neg[:], in_=page_max[h][:], axis=AXIS.X, op=ALU.max, negate=True)
-            neg_max.append(neg)
 
         page_sum = [sbuf("page_sum%d" % h, [P, PAGES], F32) for h in range(HALVES)]
         sums = [bank(6 + h, "sums%d" % h) for h in range(HALVES)]
@@ -204,12 +209,13 @@ def tile_attend_pkv4q_soft_kb_kernel(
             probs = sbuf("probs%d_%d" % (h, e), [P, PACK, P], F32)
             nc.scalar.activation(
                 out=probs[:],
-                in_=scores[h][e][:].rearrange("q (s r) -> q r s", r=PACK),
+                in_=negated[h][e][:],
                 func=ACT.Exp,
+                scale=-1.0,
                 bias=neg_max[h][:],
                 accum_out=page_sum[h][:, e : e + 1],
             )
-            turned = bank(h * PAGES + e, "probs_turned%d_%d" % (h, e))
+            turned = bank(2 * e + h, "probs_turned%d_%d" % (h, e))
             for r in range(PACK):
                 nc.tensor.transpose(turned[:, r * P : (r + 1) * P], probs[:, r, :], ident[:])
             weights = sbuf("weights%d_%d" % (h, e), [P, P, PACK], BF16)
@@ -239,7 +245,8 @@ def tile_attend_pkv4q_soft_kb_kernel(
 
         def finish(h):
             total = sbuf("total%d" % h, [P, 1], F32)
-            nc.vector.tensor_reduce(out=total[:], in_=page_sum[h][:], axis=AXIS.X, op=ALU.add)
+            copied = sbuf("copied%d" % h, [P, PAGES], F32)
+            nc.scalar.activation(out=copied[:], in_=page_sum[h][:], func=ACT.Identity, accum_out=total[:])
             inverse = sbuf("inverse%d" % h, [P, 1], F32)
             nc.vector.reciprocal(inverse[:], total[:])
             result = sbuf("result%d" % h, [P, DV], F32)

@@ -203,7 +203,7 @@ def tile_attend_pkv4q_soft_kb_kernel(
         nc.vector.tensor_copy(vw[:], vw_pool[:].indirect(voffsets[:]))
 
         page_sum = [sbuf("page_sum%d" % h, [P, PAGES], F32) for h in range(HALVES)]
-        sums = [bank(6 + h, "sums%d" % h) for h in range(HALVES)]
+        sums = [None] * HALVES
 
         def weigh(h, e):
             probs = sbuf("probs%d_%d" % (h, e), [P, PACK, P], F32)
@@ -227,12 +227,15 @@ def tile_attend_pkv4q_soft_kb_kernel(
             )
             return weights
 
-        def multiply(h, e, weights):
+        def quantise(h, e, weights):
             codes = sbuf("w_codes%d_%d" % (h, e), [P, P], U32)
             plane = sbuf("w_plane%d_%d" % (h, e), [P, P], U8)
             nc.vector.quantize_mx(
                 out=codes[:].bitcast(FP8X4), scales=plane[:], in_=weights[:].rearrange("s q r -> s (q r)")
             )
+            return codes, plane
+
+        def multiply(h, e, codes, plane):
             nc.tensor.matmul_mx(
                 out=sums[h][:, 0:DV],
                 lhsT=codes[:].bitcast(FP8X4),
@@ -254,13 +257,16 @@ def tile_attend_pkv4q_soft_kb_kernel(
             nc.sync.dma_start(out[0, h * P : (h + 1) * P, :], result[:])
 
         steps = [(h, e) for h in range(HALVES) for e in range(PAGES)]
+        quantised = {}
         pending = None
         for h, e in steps:
             weights = weigh(h, e)
             if pending is not None:
-                multiply(*pending)
-                if pending[1] == PAGES - 1:
-                    finish(pending[0])
+                quantised[pending[:2]] = quantise(*pending)
             pending = (h, e, weights)
-        multiply(*pending)
-        finish(pending[0])
+        quantised[pending[:2]] = quantise(*pending)
+        for h in range(HALVES):
+            sums[h] = bank(2 * h + 1, "sums%d" % h)
+            for e in range(PAGES):
+                multiply(h, e, *quantised[(h, e)])
+            finish(h)

@@ -28,6 +28,7 @@ HALVES = NQ // P
 TILES = PAGE // P
 QUADS = 4
 LIST_ROW = 16
+SCORE_BANK = (0, 2, 6)
 
 
 def tile_attend_pkv4q_soft_kb_kernel(
@@ -44,58 +45,55 @@ def tile_attend_pkv4q_soft_kb_kernel(
         def bank(index, name):
             return psum.tile([P, PAGE], F32, name=name, tag="bank%d" % index)
 
+        shared = ctx.enter_context(tc.tile_pool(name="shared", bufs=1))
+
+        def placed(name, shape, dtype, offset):
+            return shared.tile(shape, dtype, name=name, align_bytes=64, offset=offset)
+
+        ks_at = 4 * T
+        kb_at = ks_at + 2 * T
         offsets = keep.tile([P, N // LIST_ROW], U16, name="offsets")
         voffsets = keep.tile([P, PAGES * DV // LIST_ROW], U16, name="voffsets")
-        kw_pool = sbuf("kw_pool", [P, T], U32, "keys_then_values")
-        ks_pool = sbuf("ks_pool", [P, T], U8)
-        vsc_pool = sbuf("vsc_pool", [P, POOL_PAGES * DV], U8)
-        kb_pool = sbuf("kb_pool", [P, T], F32)
+        kw_pool = sbuf("kw_pool", [P, T], U32)
+        ks_pool = placed("ks_pool", [P, T], U8, ks_at)
+        kb_pool = placed("kb_pool", [P, T], F32, kb_at)
         qs = sbuf("qs", [P, PASSES * NQ], U8)
-        k_planes = sbuf("k_planes", [P, PASSES * N], U8)
+        ident = sbuf("ident", [P, P], F32)
 
+        nc.gpsimd.memset(qs[:].bitcast(I32), 0)
+        make_identity(nc, ident[:])
+        nc.vector.memset(kb_pool[:], 0.0)
         nc.vector.memset(ks_pool[32:64, :].bitcast(I32), 0)
         nc.vector.memset(ks_pool[64:128, :].bitcast(I32), 0)
-        nc.gpsimd.memset(vsc_pool[:].bitcast(I32), 0)
-        nc.gpsimd.memset(k_planes[:].bitcast(I32), 0)
-        nc.gpsimd.memset(qs[:].bitcast(I32), 0)
-        nc.gpsimd.memset(kb_pool[:], 0.0)
 
-        nc.sync.dma_start(ks_pool[0:32, :].bitcast(I32), k_scales.rearrange("o f t -> f o t").bitcast(I32))
         nc.sync.dma_start(offsets[:], offs)
-        nc.sync.dma_start(kw_pool[:].bitcast(I32), k_words[0].rearrange("p t b -> p (t b)").bitcast(I32))
         nc.sync.dma_start(voffsets[:], voffs)
-        qw = sbuf("qw", [P, PASSES * NQ], U32)
-        nc.sync.dma_start(
-            qw[:].bitcast(I32).rearrange("p (o q) -> p o q", o=PASSES),
-            q_words[0].rearrange("o p q r -> p o (q r)").bitcast(I32),
-        )
-        nc.sync.dma_start(
-            vsc_pool[0:16, :].bitcast(I32).rearrange("f (u e) -> f u e", u=POOL_PAGES),
-            v_scales.rearrange("u f e -> f u e").bitcast(I32),
-        )
+        nc.sync.dma_start(ks_pool[0:32, :].bitcast(I32), k_scales.rearrange("o f t -> f o t").bitcast(I32))
         for quad in range(QUADS):
             nc.sync.dma_start(
                 qs[32 * quad : 32 * quad + 4, :].bitcast(I32).rearrange("f (o q) -> f o q", o=PASSES),
                 q_scales[0, :, 4 * quad : 4 * quad + 4, :].rearrange("o f q -> f o q").bitcast(I32),
             )
+        nc.sync.dma_start(kw_pool[:].bitcast(I32), k_words[0].rearrange("p t b -> p (t b)").bitcast(I32))
+        qw = sbuf("qw", [P, PASSES * NQ], U32)
+        nc.sync.dma_start(
+            qw[:].bitcast(I32).rearrange("p (o q) -> p o q", o=PASSES),
+            q_words[0].rearrange("o p q r -> p o (q r)").bitcast(I32),
+        )
+        nc.scalar.dma_start(kb_pool[0:1, :], kb[0:1, :])
 
         ks_rows = sbuf("ks_rows", [P, N], U8)
         nc.vector.tensor_copy(ks_rows[:], ks_pool[:].indirect(offsets[:]))
+        k_planes = placed("k_planes", [P, PASSES * N], U8, ks_at + 64)
         for quad in range(QUADS):
             nc.sync.dma_start(
                 k_planes[32 * quad : 32 * quad + 4, :].bitcast(I32).rearrange("f (o n) -> f o n", o=PASSES),
                 ks_rows[8 * quad : 8 * quad + 8, :].bitcast(I32),
             )
-        nc.scalar.dma_start(kb_pool[0:1, :], kb[0:1, :])
-
-        vsc_rows = sbuf("vsc_rows", [P, PAGES * DV], U8)
-        nc.vector.tensor_copy(vsc_rows[:], vsc_pool[:].indirect(voffsets[:]))
-        vsc = sbuf("vsc", [P, PAGES * DV], U8)
-        nc.gpsimd.memset(vsc[:].bitcast(I32), 0)
-        for quad in range(QUADS):
-            nc.sync.dma_start(
-                vsc[32 * quad : 32 * quad + 4, :].bitcast(I32), vsc_rows[4 * quad : 4 * quad + 4, :].bitcast(I32)
-            )
+        vs_pool = placed("vs_pool", [P, T], F32, 64)
+        nc.sync.dma_start(vs_pool[:], vs)
+        vsc_at = ks_at + 64 + PASSES * N
+        vsc_pool = placed("vsc_pool", [P, POOL_PAGES * DV], U8, vsc_at)
 
         def page_offsets(e):
             cols = PAGE // LIST_ROW
@@ -104,7 +102,7 @@ def tile_attend_pkv4q_soft_kb_kernel(
         def bias_columns(e):
             row = sbuf("kb_row%d" % e, [P, PAGE], F32)
             nc.vector.tensor_copy(row[:], kb_pool[:].indirect(page_offsets(e)))
-            turned = bank((0, 1, 0)[e], "kb_turned%d" % e)
+            turned = bank(e, "kb_turned%d" % e)
             for j in range(TILES):
                 nc.tensor.transpose(turned[:, j * P : (j + 1) * P], row[:, j * P : (j + 1) * P], ident[:])
             cols = sbuf("kb_cols%d" % e, [P, TILES], F32)
@@ -116,7 +114,7 @@ def tile_attend_pkv4q_soft_kb_kernel(
         neg_max = [None] * HALVES
 
         def gather_keys(e):
-            pairs = sbuf("k_pairs%d" % e, [P, PAGE], U32, "pairs%d" % e)
+            pairs = placed("k_pairs%d" % e, [P, PAGE], U32, kb_at + 4 * PAGE * e)
             nc.vector.tensor_copy(pairs[:], kw_pool[:].indirect(page_offsets(e)))
             words = sbuf("k_parted%d" % e, [P, PASSES, PAGE], U16, "parted%d" % e)
             nc.vector.tensor_copy(words[:], pairs[:].bitcast(U16).rearrange("p (n o) -> p o n", o=PASSES))
@@ -125,7 +123,7 @@ def tile_attend_pkv4q_soft_kb_kernel(
         def raw_scores(e, words):
             raws = []
             for pair in range(TILES // 2):
-                raw = bank(2 + 2 * e + pair, "raw%d_%d" % (e, pair))
+                raw = bank(4 + 2 * (e % 2) + pair, "raw%d_%d" % (e, pair))
                 raws.append(raw)
                 for jj in range(2):
                     j = 2 * pair + jj
@@ -146,7 +144,7 @@ def tile_attend_pkv4q_soft_kb_kernel(
 
         def biased_scores(e, raws, kb_cols):
             for h in range(HALVES):
-                scores[h][e] = bank(2 * e + h, "score%d_%d" % (h, e))
+                scores[h][e] = bank(SCORE_BANK[e] + h, "score%d_%d" % (h, e))
             for j in range(TILES):
                 biased = sbuf("biased%d_%d" % (e, j), [P, NQ], F32)
                 nc.scalar.activation(
@@ -159,7 +157,7 @@ def tile_attend_pkv4q_soft_kb_kernel(
                     nc.tensor.transpose(scores[h][e][:, j * P : (j + 1) * P], biased[:, h * P : (h + 1) * P], ident[:])
 
         def max_page(h, e):
-            negated[h][e] = sbuf("negated%d_%d" % (h, e), [P, PACK, P], F32)
+            negated[h][e] = placed("negated%d_%d" % (h, e), [P, PACK, P], F32, negated_at[h][e])
             least = sbuf("neg_max%d_%d" % (h, e), [P, 1], F32, "neg_max%d_%d" % (h, e))
             nc.vector.tensor_scalar(
                 out=negated[h][e][:],
@@ -172,20 +170,35 @@ def tile_attend_pkv4q_soft_kb_kernel(
             )
             neg_max[h] = least
 
-        raws = [raw_scores(e, gather_keys(e)) for e in range(PAGES)]
-        ident = sbuf("ident", [P, P], F32, "parted0")
-        make_identity(nc, ident[:])
         kb_cols = [bias_columns(e) for e in range(PAGES)]
-        for e in range(PAGES):
-            biased_scores(e, raws[e], kb_cols[e])
-
-        vs_pool = sbuf("vs_pool", [P, T], F32, "pairs0")
-        nc.scalar.dma_start(vs_pool[:], vs)
-        vw_pool = sbuf("vw_pool", [P, POOL_PAGES * DV], U32, "keys_then_values")
-        nc.scalar.dma_start(
+        nc.vector.memset(vsc_pool[:].bitcast(I32), 0)
+        nc.sync.dma_start(
+            vsc_pool[0:16, :].bitcast(I32).rearrange("f (u e) -> f u e", u=POOL_PAGES),
+            v_scales.rearrange("u f e -> f u e").bitcast(I32),
+        )
+        vw_pool = placed("vw_pool", [P, POOL_PAGES * DV], U32, kb_at + 4 * PAGE * PAGES)
+        nc.sync.dma_start(
             vw_pool[:].bitcast(I32).rearrange("p (u e) -> p u e", u=POOL_PAGES),
             v_words.rearrange("u p e r -> p u (e r)").bitcast(I32),
         )
+        words = [gather_keys(e) for e in range(PAGES)]
+        raws = [raw_scores(e, words[e]) for e in range(2)]
+        biased_scores(0, raws[0], kb_cols[0])
+        raws.append(raw_scores(2, words[2]))
+        biased_scores(1, raws[1], kb_cols[1])
+        biased_scores(2, raws[2], kb_cols[2])
+
+        vsc_rows = sbuf("vsc_rows", [P, PAGES * DV], U8)
+        nc.vector.tensor_copy(vsc_rows[:], vsc_pool[:].indirect(voffsets[:]))
+        vsc = placed("vsc", [P, PAGES * DV], U8, vsc_at)
+        for quad in range(QUADS):
+            nc.sync.dma_start(
+                vsc[32 * quad : 32 * quad + 4, :].bitcast(I32), vsc_rows[4 * quad : 4 * quad + 4, :].bitcast(I32)
+            )
+
+        free_at = kb_at + 4 * T
+        negated_at = [[free_at + 4 * PAGE * (PAGES * h + e) for e in range(PAGES)] for h in range(HALVES)]
+        negated_at[0][1] = 64
 
         vs_row = sbuf("vs_row", [P, N], F32)
         nc.vector.tensor_copy(vs_row[:], vs_pool[:].indirect(offsets[:]))
@@ -215,7 +228,7 @@ def tile_attend_pkv4q_soft_kb_kernel(
                 bias=neg_max[h][:],
                 accum_out=page_sum[h][:, e : e + 1],
             )
-            turned = bank(2 * e + h, "probs_turned%d_%d" % (h, e))
+            turned = bank(SCORE_BANK[e] + h, "probs_turned%d_%d" % (h, e))
             for r in range(PACK):
                 nc.tensor.transpose(turned[:, r * P : (r + 1) * P], probs[:, r, :], ident[:])
             weights = sbuf("weights%d_%d" % (h, e), [P, P, PACK], BF16)
@@ -266,7 +279,7 @@ def tile_attend_pkv4q_soft_kb_kernel(
             pending = (h, e, weights)
         quantised[pending[:2]] = quantise(*pending)
         for h in range(HALVES):
-            sums[h] = bank(2 * h + 1, "sums%d" % h)
+            sums[h] = bank(3 + h, "sums%d" % h)
             for e in range(PAGES):
                 multiply(h, e, *quantised[(h, e)])
             finish(h)

@@ -60,15 +60,27 @@ def tile_attend_pkv4q_soft_kb_kernel(
         qs = sbuf("qs", [P, PASSES * NQ], U8)
         ident = sbuf("ident", [P, P], F32)
 
-        nc.gpsimd.memset(qs[:].bitcast(I32), 0)
-        make_identity(nc, ident[:])
-        nc.vector.memset(kb_pool[:], 0.0)
-        nc.vector.memset(ks_pool[32:64, :].bitcast(I32), 0)
-        nc.vector.memset(ks_pool[64:128, :].bitcast(I32), 0)
+        vsc_pool = sbuf("vsc_pool", [P, POOL_PAGES * DV], U8, "value_scales")
 
+        def clear(words):
+            last = words.shape[1] - 1
+            nc.vector.memset(words[:, 0:last], 0)
+            nc.vector.memset(words[:, last:], 0)
+
+        nc.gpsimd.memset(vsc_pool[:].bitcast(I32), 0)
+        nc.gpsimd.memset(kb_pool[:], 0.0)
+        make_identity(nc, ident[:])
+        nc.gpsimd.memset(qs[:].bitcast(I32), 0)
+        clear(ks_pool[32:64, :].bitcast(I32))
+        clear(ks_pool[64:128, :].bitcast(I32))
+
+        nc.sync.dma_start(ks_pool[0:32, :].bitcast(I32), k_scales.rearrange("o f t -> f o t").bitcast(I32))
         nc.sync.dma_start(offsets[:], offs)
         nc.sync.dma_start(voffsets[:], voffs)
-        nc.sync.dma_start(ks_pool[0:32, :].bitcast(I32), k_scales.rearrange("o f t -> f o t").bitcast(I32))
+        nc.sync.dma_start(
+            vsc_pool[0:16, :].bitcast(I32).rearrange("f (u e) -> f u e", u=POOL_PAGES),
+            v_scales.rearrange("u f e -> f u e").bitcast(I32),
+        )
         for quad in range(QUADS):
             nc.sync.dma_start(
                 qs[32 * quad : 32 * quad + 4, :].bitcast(I32).rearrange("f (o q) -> f o q", o=PASSES),
@@ -92,15 +104,21 @@ def tile_attend_pkv4q_soft_kb_kernel(
             )
         vs_pool = placed("vs_pool", [P, T], F32, 64)
         nc.sync.dma_start(vs_pool[:], vs)
-        vsc_at = ks_at + 64 + PASSES * N
-        vsc_pool = placed("vsc_pool", [P, POOL_PAGES * DV], U8, vsc_at)
+
+        vsc_rows = sbuf("vsc_rows", [P, PAGES * DV], U8)
+        nc.vector.tensor_copy(vsc_rows[:], vsc_pool[:].indirect(voffsets[:]))
+        vsc = sbuf("vsc", [P, PAGES * DV], U8, "value_scales")
+        for quad in range(QUADS):
+            nc.sync.dma_start(
+                vsc[32 * quad : 32 * quad + 4, :].bitcast(I32), vsc_rows[4 * quad : 4 * quad + 4, :].bitcast(I32)
+            )
 
         def page_offsets(e):
             cols = PAGE // LIST_ROW
             return offsets[:, e * cols : (e + 1) * cols]
 
         def bias_columns(e):
-            row = sbuf("kb_row%d" % e, [P, PAGE], F32)
+            row = sbuf("kb_row%d" % e, [P, PAGE], F32, "page%d" % e)
             nc.vector.tensor_copy(row[:], kb_pool[:].indirect(page_offsets(e)))
             turned = bank(e, "kb_turned%d" % e)
             for j in range(TILES):
@@ -114,7 +132,7 @@ def tile_attend_pkv4q_soft_kb_kernel(
         neg_max = [None] * HALVES
 
         def gather_keys(e):
-            pairs = placed("k_pairs%d" % e, [P, PAGE], U32, kb_at + 4 * PAGE * e)
+            pairs = sbuf("k_pairs%d" % e, [P, PAGE], U32, "page%d" % e)
             nc.vector.tensor_copy(pairs[:], kw_pool[:].indirect(page_offsets(e)))
             words = sbuf("k_parted%d" % e, [P, PASSES, PAGE], U16, "parted%d" % e)
             nc.vector.tensor_copy(words[:], pairs[:].bitcast(U16).rearrange("p (n o) -> p o n", o=PASSES))
@@ -171,12 +189,7 @@ def tile_attend_pkv4q_soft_kb_kernel(
             neg_max[h] = least
 
         kb_cols = [bias_columns(e) for e in range(PAGES)]
-        nc.vector.memset(vsc_pool[:].bitcast(I32), 0)
-        nc.sync.dma_start(
-            vsc_pool[0:16, :].bitcast(I32).rearrange("f (u e) -> f u e", u=POOL_PAGES),
-            v_scales.rearrange("u f e -> f u e").bitcast(I32),
-        )
-        vw_pool = placed("vw_pool", [P, POOL_PAGES * DV], U32, kb_at + 4 * PAGE * PAGES)
+        vw_pool = placed("vw_pool", [P, POOL_PAGES * DV], U32, kb_at)
         nc.sync.dma_start(
             vw_pool[:].bitcast(I32).rearrange("p (u e) -> p u e", u=POOL_PAGES),
             v_words.rearrange("u p e r -> p u (e r)").bitcast(I32),
@@ -188,17 +201,10 @@ def tile_attend_pkv4q_soft_kb_kernel(
         biased_scores(1, raws[1], kb_cols[1])
         biased_scores(2, raws[2], kb_cols[2])
 
-        vsc_rows = sbuf("vsc_rows", [P, PAGES * DV], U8)
-        nc.vector.tensor_copy(vsc_rows[:], vsc_pool[:].indirect(voffsets[:]))
-        vsc = placed("vsc", [P, PAGES * DV], U8, vsc_at)
-        for quad in range(QUADS):
-            nc.sync.dma_start(
-                vsc[32 * quad : 32 * quad + 4, :].bitcast(I32), vsc_rows[4 * quad : 4 * quad + 4, :].bitcast(I32)
-            )
-
         free_at = kb_at + 4 * T
         negated_at = [[free_at + 4 * PAGE * (PAGES * h + e) for e in range(PAGES)] for h in range(HALVES)]
-        negated_at[0][1] = 64
+        negated_at[0][0] = 64
+        negated_at[1][0] = 64 + 4 * PAGE
 
         vs_row = sbuf("vs_row", [P, N], F32)
         nc.vector.tensor_copy(vs_row[:], vs_pool[:].indirect(offsets[:]))

@@ -67,20 +67,18 @@ def tile_attend_pkv4q_soft_kb_kernel(
             nc.vector.memset(words[:, 0:last], 0)
             nc.vector.memset(words[:, last:], 0)
 
-        nc.gpsimd.memset(vsc_pool[:].bitcast(I32), 0)
+        zeros = sbuf("zeros", [P, PAGE], F32)
         nc.gpsimd.memset(kb_pool[:], 0.0)
+        nc.gpsimd.memset(zeros[:], 0.0)
         make_identity(nc, ident[:])
         nc.gpsimd.memset(qs[:].bitcast(I32), 0)
+        nc.gpsimd.memset(vsc_pool[:].bitcast(I32), 0)
         clear(ks_pool[32:64, :].bitcast(I32))
         clear(ks_pool[64:128, :].bitcast(I32))
 
         nc.sync.dma_start(ks_pool[0:32, :].bitcast(I32), k_scales.rearrange("o f t -> f o t").bitcast(I32))
         nc.sync.dma_start(offsets[:], offs)
         nc.sync.dma_start(voffsets[:], voffs)
-        nc.sync.dma_start(
-            vsc_pool[0:16, :].bitcast(I32).rearrange("f (u e) -> f u e", u=POOL_PAGES),
-            v_scales.rearrange("u f e -> f u e").bitcast(I32),
-        )
         for quad in range(QUADS):
             nc.sync.dma_start(
                 qs[32 * quad : 32 * quad + 4, :].bitcast(I32).rearrange("f (o q) -> f o q", o=PASSES),
@@ -102,16 +100,12 @@ def tile_attend_pkv4q_soft_kb_kernel(
                 k_planes[32 * quad : 32 * quad + 4, :].bitcast(I32).rearrange("f (o n) -> f o n", o=PASSES),
                 ks_rows[8 * quad : 8 * quad + 8, :].bitcast(I32),
             )
+        nc.sync.dma_start(
+            vsc_pool[0:16, :].bitcast(I32).rearrange("f (u e) -> f u e", u=POOL_PAGES),
+            v_scales.rearrange("u f e -> f u e").bitcast(I32),
+        )
         vs_pool = placed("vs_pool", [P, T], F32, 64)
         nc.sync.dma_start(vs_pool[:], vs)
-
-        vsc_rows = sbuf("vsc_rows", [P, PAGES * DV], U8)
-        nc.vector.tensor_copy(vsc_rows[:], vsc_pool[:].indirect(voffsets[:]))
-        vsc = sbuf("vsc", [P, PAGES * DV], U8, "value_scales")
-        for quad in range(QUADS):
-            nc.sync.dma_start(
-                vsc[32 * quad : 32 * quad + 4, :].bitcast(I32), vsc_rows[4 * quad : 4 * quad + 4, :].bitcast(I32)
-            )
 
         def page_offsets(e):
             cols = PAGE // LIST_ROW
@@ -119,7 +113,7 @@ def tile_attend_pkv4q_soft_kb_kernel(
 
         def bias_columns(e):
             row = sbuf("kb_row%d" % e, [P, PAGE], F32, "page%d" % e)
-            nc.vector.tensor_copy(row[:], kb_pool[:].indirect(page_offsets(e)))
+            nc.vector.tensor_tensor(out=row[:], in0=kb_pool[:].indirect(page_offsets(e)), in1=zeros[:], op=ALU.add)
             turned = bank(e, "kb_turned%d" % e)
             for j in range(TILES):
                 nc.tensor.transpose(turned[:, j * P : (j + 1) * P], row[:, j * P : (j + 1) * P], ident[:])
@@ -201,17 +195,25 @@ def tile_attend_pkv4q_soft_kb_kernel(
         biased_scores(1, raws[1], kb_cols[1])
         biased_scores(2, raws[2], kb_cols[2])
 
+        vsc_rows = sbuf("vsc_rows", [P, PAGES * DV], U8, "page1")
+        nc.vector.tensor_copy(vsc_rows[:], vsc_pool[:].indirect(voffsets[:]))
+        vsc = sbuf("vsc", [P, PAGES * DV], U8, "value_scales")
+        for quad in range(QUADS):
+            nc.sync.dma_start(
+                vsc[32 * quad : 32 * quad + 4, :].bitcast(I32), vsc_rows[4 * quad : 4 * quad + 4, :].bitcast(I32)
+            )
+
         free_at = kb_at + 4 * T
         negated_at = [[free_at + 4 * PAGE * (PAGES * h + e) for e in range(PAGES)] for h in range(HALVES)]
         negated_at[0][0] = 64
         negated_at[1][0] = 64 + 4 * PAGE
 
-        vs_row = sbuf("vs_row", [P, N], F32)
-        nc.vector.tensor_copy(vs_row[:], vs_pool[:].indirect(offsets[:]))
         vs_cols = []
         for e in range(PAGES):
+            vs_row = sbuf("vs_row%d" % e, [P, PAGE], F32)
+            nc.vector.tensor_tensor(out=vs_row[:], in0=vs_pool[:].indirect(page_offsets(e)), in1=zeros[:], op=ALU.add)
             cols = sbuf("vs_cols%d" % e, [P, PACK], F32)
-            nc.sync.dma_start(cols[:], vs_row[0:1, e * PAGE : (e + 1) * PAGE])
+            nc.sync.dma_start(cols[:], vs_row[0:1, :])
             vs_cols.append(cols)
 
         for e in range(PAGES):

@@ -28,7 +28,10 @@ HALVES = NQ // P
 TILES = PAGE // P
 QUADS = 4
 LIST_ROW = 16
-SCORE_BANK = (0, 2, 6)
+SCORE_BANK = (6, 0, 2)
+SUM_BANK = (7, 2)
+BIAS_BANK = (6, 7, 4)
+TURN_BANK = ((4, 6, 0), (5, 7, 1))
 
 
 def tile_attend_pkv4q_soft_kb_kernel(
@@ -50,8 +53,12 @@ def tile_attend_pkv4q_soft_kb_kernel(
         def placed(name, shape, dtype, offset):
             return shared.tile(shape, dtype, name=name, align_bytes=64, offset=offset)
 
-        ks_at = 4 * T
+        vs_at = 0
+        ks_at = vs_at + 4 * T - 64
+        qw_at = ks_at + 64 + PASSES * N
         kb_at = ks_at + 2 * T
+        vw_at = kb_at + 2 * T
+        rows_at = 96
         offsets = keep.tile([P, N // LIST_ROW], U16, name="offsets")
         voffsets = keep.tile([P, PAGES * DV // LIST_ROW], U16, name="voffsets")
         kw_pool = sbuf("kw_pool", [P, T], U32)
@@ -59,36 +66,26 @@ def tile_attend_pkv4q_soft_kb_kernel(
         kb_pool = placed("kb_pool", [P, T], F32, kb_at)
         qs = sbuf("qs", [P, PASSES * NQ], U8)
         ident = sbuf("ident", [P, P], F32)
-
         vsc_pool = sbuf("vsc_pool", [P, POOL_PAGES * DV], U8, "value_scales")
 
-        def clear(words):
-            last = words.shape[1] - 1
-            nc.vector.memset(words[:, 0:last], 0)
-            nc.vector.memset(words[:, last:], 0)
-
-        zeros = sbuf("zeros", [P, PAGE], F32)
-        nc.gpsimd.memset(kb_pool[:], 0.0)
-        nc.gpsimd.memset(zeros[:], 0.0)
+        nc.vector.memset(qs[:].bitcast(I32), 0)
+        nc.vector.memset(kb_pool[:], 0.0)
+        nc.vector.memset(ks_pool[0:rows_at, :].bitcast(I32), 0)
         make_identity(nc, ident[:])
-        nc.gpsimd.memset(qs[:].bitcast(I32), 0)
         nc.gpsimd.memset(vsc_pool[:].bitcast(I32), 0)
-        clear(ks_pool[32:64, :].bitcast(I32))
-        clear(ks_pool[64:128, :].bitcast(I32))
 
-        nc.sync.dma_start(ks_pool[0:32, :].bitcast(I32), k_scales.rearrange("o f t -> f o t").bitcast(I32))
         nc.sync.dma_start(offsets[:], offs)
+        nc.sync.dma_start(ks_pool[rows_at:P, :].bitcast(I32), k_scales.rearrange("o f t -> f o t").bitcast(I32))
+        nc.sync.dma_start(kw_pool[:].bitcast(I32), k_words[0].rearrange("p t b -> p (t b)").bitcast(I32))
         nc.sync.dma_start(voffsets[:], voffs)
         for quad in range(QUADS):
-            nc.sync.dma_start(
+            nc.scalar.dma_start(
                 qs[32 * quad : 32 * quad + 4, :].bitcast(I32).rearrange("f (o q) -> f o q", o=PASSES),
                 q_scales[0, :, 4 * quad : 4 * quad + 4, :].rearrange("o f q -> f o q").bitcast(I32),
             )
-        nc.sync.dma_start(kw_pool[:].bitcast(I32), k_words[0].rearrange("p t b -> p (t b)").bitcast(I32))
-        qw = sbuf("qw", [P, PASSES * NQ], U32)
         nc.sync.dma_start(
-            qw[:].bitcast(I32).rearrange("p (o q) -> p o q", o=PASSES),
-            q_words[0].rearrange("o p q r -> p o (q r)").bitcast(I32),
+            vsc_pool[0:16, :].bitcast(I32).rearrange("f (u e) -> f u e", u=POOL_PAGES),
+            v_scales.rearrange("u f e -> f u e").bitcast(I32),
         )
         nc.scalar.dma_start(kb_pool[0:1, :], kb[0:1, :])
 
@@ -96,15 +93,16 @@ def tile_attend_pkv4q_soft_kb_kernel(
         nc.vector.tensor_copy(ks_rows[:], ks_pool[:].indirect(offsets[:]))
         k_planes = placed("k_planes", [P, PASSES * N], U8, ks_at + 64)
         for quad in range(QUADS):
-            nc.sync.dma_start(
+            nc.scalar.dma_start(
                 k_planes[32 * quad : 32 * quad + 4, :].bitcast(I32).rearrange("f (o n) -> f o n", o=PASSES),
-                ks_rows[8 * quad : 8 * quad + 8, :].bitcast(I32),
+                ks_rows[rows_at + 8 * quad : rows_at + 8 * quad + 8, :].bitcast(I32),
             )
+        qw = placed("qw", [P, PASSES * NQ], U32, qw_at)
         nc.sync.dma_start(
-            vsc_pool[0:16, :].bitcast(I32).rearrange("f (u e) -> f u e", u=POOL_PAGES),
-            v_scales.rearrange("u f e -> f u e").bitcast(I32),
+            qw[:].bitcast(I32).rearrange("p (o q) -> p o q", o=PASSES),
+            q_words[0].rearrange("o p q r -> p o (q r)").bitcast(I32),
         )
-        vs_pool = placed("vs_pool", [P, T], F32, 64)
+        vs_pool = placed("vs_pool", [P, T], F32, vs_at)
         nc.sync.dma_start(vs_pool[:], vs)
 
         def page_offsets(e):
@@ -112,13 +110,13 @@ def tile_attend_pkv4q_soft_kb_kernel(
             return offsets[:, e * cols : (e + 1) * cols]
 
         def bias_columns(e):
-            row = sbuf("kb_row%d" % e, [P, PAGE], F32, "page%d" % e)
-            nc.vector.tensor_tensor(out=row[:], in0=kb_pool[:].indirect(page_offsets(e)), in1=zeros[:], op=ALU.add)
-            turned = bank(e, "kb_turned%d" % e)
+            row = sbuf("kb_row%d" % e, [P, PAGE], F32)
+            nc.vector.tensor_copy(row[:], kb_pool[:].indirect(page_offsets(e)))
+            turned = bank(BIAS_BANK[e], "kb_turned%d" % e)
             for j in range(TILES):
                 nc.tensor.transpose(turned[:, j * P : (j + 1) * P], row[:, j * P : (j + 1) * P], ident[:])
             cols = sbuf("kb_cols%d" % e, [P, TILES], F32)
-            nc.scalar.copy(cols[:], turned[:, 0:PAGE:P])
+            nc.scalar.activation(out=cols[:], in_=turned[:, 0:PAGE:P], func=ACT.Copy)
             return cols
 
         scores = [[None] * PAGES for h in range(HALVES)]
@@ -126,7 +124,7 @@ def tile_attend_pkv4q_soft_kb_kernel(
         neg_max = [None] * HALVES
 
         def gather_keys(e):
-            pairs = sbuf("k_pairs%d" % e, [P, PAGE], U32, "page%d" % e)
+            pairs = placed("k_pairs%d" % e, [P, PAGE], U32, kb_at + 4 * PAGE * e)
             nc.vector.tensor_copy(pairs[:], kw_pool[:].indirect(page_offsets(e)))
             words = sbuf("k_parted%d" % e, [P, PASSES, PAGE], U16, "parted%d" % e)
             nc.vector.tensor_copy(words[:], pairs[:].bitcast(U16).rearrange("p (n o) -> p o n", o=PASSES))
@@ -135,7 +133,7 @@ def tile_attend_pkv4q_soft_kb_kernel(
         def raw_scores(e, words):
             raws = []
             for pair in range(TILES // 2):
-                raw = bank(4 + 2 * (e % 2) + pair, "raw%d_%d" % (e, pair))
+                raw = bank(2 * e + pair, "raw%d_%d" % (e, pair))
                 raws.append(raw)
                 for jj in range(2):
                     j = 2 * pair + jj
@@ -183,7 +181,7 @@ def tile_attend_pkv4q_soft_kb_kernel(
             neg_max[h] = least
 
         kb_cols = [bias_columns(e) for e in range(PAGES)]
-        vw_pool = placed("vw_pool", [P, POOL_PAGES * DV], U32, kb_at)
+        vw_pool = placed("vw_pool", [P, POOL_PAGES * DV], U32, vw_at)
         nc.sync.dma_start(
             vw_pool[:].bitcast(I32).rearrange("p (u e) -> p u e", u=POOL_PAGES),
             v_words.rearrange("u p e r -> p u (e r)").bitcast(I32),
@@ -195,7 +193,7 @@ def tile_attend_pkv4q_soft_kb_kernel(
         biased_scores(1, raws[1], kb_cols[1])
         biased_scores(2, raws[2], kb_cols[2])
 
-        vsc_rows = sbuf("vsc_rows", [P, PAGES * DV], U8, "page1")
+        vsc_rows = placed("vsc_rows", [P, PAGES * DV], U8, kb_at + 4 * PAGE)
         nc.vector.tensor_copy(vsc_rows[:], vsc_pool[:].indirect(voffsets[:]))
         vsc = sbuf("vsc", [P, PAGES * DV], U8, "value_scales")
         for quad in range(QUADS):
@@ -205,15 +203,15 @@ def tile_attend_pkv4q_soft_kb_kernel(
 
         free_at = kb_at + 4 * T
         negated_at = [[free_at + 4 * PAGE * (PAGES * h + e) for e in range(PAGES)] for h in range(HALVES)]
-        negated_at[0][0] = 64
-        negated_at[1][0] = 64 + 4 * PAGE
+        negated_at[0][0] = vs_at
+        negated_at[1][0] = vs_at + 4 * PAGE
 
+        vs_row = sbuf("vs_row", [P, N], F32)
+        nc.vector.tensor_copy(vs_row[:], vs_pool[:].indirect(offsets[:]))
         vs_cols = []
         for e in range(PAGES):
-            vs_row = sbuf("vs_row%d" % e, [P, PAGE], F32)
-            nc.vector.tensor_tensor(out=vs_row[:], in0=vs_pool[:].indirect(page_offsets(e)), in1=zeros[:], op=ALU.add)
             cols = sbuf("vs_cols%d" % e, [P, PACK], F32)
-            nc.sync.dma_start(cols[:], vs_row[0:1, :])
+            nc.sync.dma_start(cols[:], vs_row[e : e + 1, e * PAGE : (e + 1) * PAGE])
             vs_cols.append(cols)
 
         for e in range(PAGES):
@@ -236,7 +234,7 @@ def tile_attend_pkv4q_soft_kb_kernel(
                 bias=neg_max[h][:],
                 accum_out=page_sum[h][:, e : e + 1],
             )
-            turned = bank(SCORE_BANK[e] + h, "probs_turned%d_%d" % (h, e))
+            turned = bank(TURN_BANK[h][e], "probs_turned%d_%d" % (h, e))
             for r in range(PACK):
                 nc.tensor.transpose(turned[:, r * P : (r + 1) * P], probs[:, r, :], ident[:])
             weights = sbuf("weights%d_%d" % (h, e), [P, P, PACK], BF16)
@@ -287,7 +285,7 @@ def tile_attend_pkv4q_soft_kb_kernel(
             pending = (h, e, weights)
         quantised[pending[:2]] = quantise(*pending)
         for h in range(HALVES):
-            sums[h] = bank(3 + h, "sums%d" % h)
+            sums[h] = bank(SUM_BANK[h], "sums%d" % h)
             for e in range(PAGES):
                 multiply(h, e, *quantised[(h, e)])
             finish(h)

@@ -68,11 +68,16 @@ def tile_attend_pkv4q_soft_kb_kernel(
         ident = sbuf("ident", [P, P], F32)
         vsc_pool = sbuf("vsc_pool", [P, POOL_PAGES * DV], U8, "value_scales")
 
-        nc.vector.memset(qs[:].bitcast(I32), 0)
-        nc.vector.memset(kb_pool[:], 0.0)
-        nc.vector.memset(ks_pool[0:rows_at, :].bitcast(I32), 0)
+        def clear(words):
+            last = words.shape[1] - 1
+            nc.vector.memset(words[:, 0:last], 0)
+            nc.vector.memset(words[:, last:], 0)
+
+        nc.gpsimd.memset(kb_pool[:], 0.0)
         make_identity(nc, ident[:])
-        nc.gpsimd.memset(vsc_pool[:].bitcast(I32), 0)
+        clear(qs[:].bitcast(I32))
+        clear(ks_pool[0:rows_at, :].bitcast(I32))
+        clear(vsc_pool[:].bitcast(I32))
 
         nc.sync.dma_start(offsets[:], offs)
         nc.sync.dma_start(ks_pool[rows_at:P, :].bitcast(I32), k_scales.rearrange("o f t -> f o t").bitcast(I32))

@@ -84,7 +84,7 @@ def tile_attend_pkv4q_soft_kb_kernel(
         nc.sync.dma_start(kw_pool[:].bitcast(I32), k_words[0].rearrange("p t b -> p (t b)").bitcast(I32))
         nc.sync.dma_start(voffsets[:], voffs)
         for quad in range(QUADS):
-            nc.scalar.dma_start(
+            nc.sync.dma_start(
                 qs[32 * quad : 32 * quad + 4, :].bitcast(I32).rearrange("f (o q) -> f o q", o=PASSES),
                 q_scales[0, :, 4 * quad : 4 * quad + 4, :].rearrange("o f q -> f o q").bitcast(I32),
             )
@@ -98,7 +98,7 @@ def tile_attend_pkv4q_soft_kb_kernel(
         nc.vector.tensor_copy(ks_rows[:], ks_pool[:].indirect(offsets[:]))
         k_planes = placed("k_planes", [P, PASSES * N], U8, ks_at + 64)
         for quad in range(QUADS):
-            nc.scalar.dma_start(
+            nc.sync.dma_start(
                 k_planes[32 * quad : 32 * quad + 4, :].bitcast(I32).rearrange("f (o n) -> f o n", o=PASSES),
                 ks_rows[rows_at + 8 * quad : rows_at + 8 * quad + 8, :].bitcast(I32),
             )
@@ -129,9 +129,13 @@ def tile_attend_pkv4q_soft_kb_kernel(
         neg_max = [None] * HALVES
 
         def gather_keys(e):
-            pairs = placed("k_pairs%d" % e, [P, PAGE], U32, kb_at + 4 * PAGE * e)
+            if e == 0:
+                pairs = sbuf("k_pairs0", [P, PAGE], U32)
+                words = placed("k_parted0", [P, PASSES, PAGE], U16, kb_at)
+            else:
+                pairs = placed("k_pairs%d" % e, [P, PAGE], U32, kb_at + 4 * PAGE * e)
+                words = sbuf("k_parted%d" % e, [P, PASSES, PAGE], U16)
             nc.vector.tensor_copy(pairs[:], kw_pool[:].indirect(page_offsets(e)))
-            words = sbuf("k_parted%d" % e, [P, PASSES, PAGE], U16, "parted%d" % e)
             nc.vector.tensor_copy(words[:], pairs[:].bitcast(U16).rearrange("p (n o) -> p o n", o=PASSES))
             return words
 

@@ -55,7 +55,8 @@ def tile_attend_pkv4q_soft_kb_kernel(
 
         vs_at = 0
         ks_at = vs_at + 4 * T - 64
-        qw_at = ks_at + 64 + PASSES * N
+        qs_at = ks_at + 64 + PASSES * N
+        qw_at = qs_at + PASSES * NQ
         kb_at = ks_at + 2 * T
         vw_at = kb_at + 2 * T
         rows_at = 96
@@ -64,7 +65,6 @@ def tile_attend_pkv4q_soft_kb_kernel(
         kw_pool = sbuf("kw_pool", [P, T], U32)
         ks_pool = placed("ks_pool", [P, T], U8, ks_at)
         kb_pool = placed("kb_pool", [P, T], F32, kb_at)
-        qs = sbuf("qs", [P, PASSES * NQ], U8)
         ident = sbuf("ident", [P, P], F32)
         vsc_pool = sbuf("vsc_pool", [P, POOL_PAGES * DV], U8, "value_scales")
 
@@ -75,7 +75,6 @@ def tile_attend_pkv4q_soft_kb_kernel(
 
         nc.gpsimd.memset(kb_pool[:], 0.0)
         make_identity(nc, ident[:])
-        clear(qs[:].bitcast(I32))
         clear(ks_pool[0:rows_at, :].bitcast(I32))
         clear(vsc_pool[:].bitcast(I32))
 
@@ -83,11 +82,6 @@ def tile_attend_pkv4q_soft_kb_kernel(
         nc.sync.dma_start(ks_pool[rows_at:P, :].bitcast(I32), k_scales.rearrange("o f t -> f o t").bitcast(I32))
         nc.sync.dma_start(kw_pool[:].bitcast(I32), k_words[0].rearrange("p t b -> p (t b)").bitcast(I32))
         nc.sync.dma_start(voffsets[:], voffs)
-        for quad in range(QUADS):
-            nc.sync.dma_start(
-                qs[32 * quad : 32 * quad + 4, :].bitcast(I32).rearrange("f (o q) -> f o q", o=PASSES),
-                q_scales[0, :, 4 * quad : 4 * quad + 4, :].rearrange("o f q -> f o q").bitcast(I32),
-            )
         nc.sync.dma_start(
             vsc_pool[0:16, :].bitcast(I32).rearrange("f (u e) -> f u e", u=POOL_PAGES),
             v_scales.rearrange("u f e -> f u e").bitcast(I32),
@@ -107,6 +101,12 @@ def tile_attend_pkv4q_soft_kb_kernel(
             qw[:].bitcast(I32).rearrange("p (o q) -> p o q", o=PASSES),
             q_words[0].rearrange("o p q r -> p o (q r)").bitcast(I32),
         )
+        qs = placed("qs", [P, PASSES * NQ], U8, qs_at)
+        for quad in range(QUADS):
+            nc.sync.dma_start(
+                qs[32 * quad : 32 * quad + 4, :].bitcast(I32).rearrange("f (o q) -> f o q", o=PASSES),
+                q_scales[0, :, 4 * quad : 4 * quad + 4, :].rearrange("o f q -> f o q").bitcast(I32),
+            )
         vs_pool = placed("vs_pool", [P, T], F32, vs_at)
         nc.sync.dma_start(vs_pool[:], vs)
 
@@ -196,11 +196,9 @@ def tile_attend_pkv4q_soft_kb_kernel(
             v_words.rearrange("u p e r -> p u (e r)").bitcast(I32),
         )
         words = [gather_keys(e) for e in range(PAGES)]
-        raws = [raw_scores(e, words[e]) for e in range(2)]
-        biased_scores(0, raws[0], kb_cols[0])
-        raws.append(raw_scores(2, words[2]))
-        biased_scores(1, raws[1], kb_cols[1])
-        biased_scores(2, raws[2], kb_cols[2])
+        raws = [raw_scores(e, words[e]) for e in range(PAGES)]
+        for e in range(PAGES):
+            biased_scores(e, raws[e], kb_cols[e])
 
         vsc_rows = placed("vsc_rows", [P, PAGES * DV], U8, kb_at + 4 * PAGE)
         nc.vector.tensor_copy(vsc_rows[:], vsc_pool[:].indirect(voffsets[:]))

@@ -28,10 +28,8 @@ HALVES = NQ // P
 TILES = PAGE // P
 QUADS = 4
 LIST_ROW = 16
-SCORE_BANK = (6, 0, 2)
-SUM_BANK = (7, 2)
-BIAS_BANK = (6, 7, 4)
-TURN_BANK = ((4, 6, 0), (5, 7, 1))
+SUM_BANK = (2, 4)
+TURN_BANK = ((6, 7, 0), (1, 2, 3))
 
 
 def tile_attend_pkv4q_soft_kb_kernel(
@@ -53,27 +51,27 @@ def tile_attend_pkv4q_soft_kb_kernel(
         def placed(name, shape, dtype, offset):
             return shared.tile(shape, dtype, name=name, align_bytes=64, offset=offset)
 
-        vs_at = 0
-        ks_at = vs_at + 4 * T - 64
+        kb_at = 0
+        ks_at = kb_at + 4 * T - 64
         qs_at = ks_at + 64 + PASSES * N
         qw_at = qs_at + PASSES * NQ
-        kb_at = ks_at + 2 * T
-        vw_at = kb_at + 2 * T
+        vs_at = ks_at + 2 * T
+        vw_at = vs_at + 2 * T
         rows_at = 96
         offsets = keep.tile([P, N // LIST_ROW], U16, name="offsets")
         voffsets = keep.tile([P, PAGES * DV // LIST_ROW], U16, name="voffsets")
         kw_pool = sbuf("kw_pool", [P, T], U32)
         ks_pool = placed("ks_pool", [P, T], U8, ks_at)
-        kb_pool = placed("kb_pool", [P, T], F32, kb_at)
+        vs_pool = placed("vs_pool", [P, T], F32, vs_at)
         ident = sbuf("ident", [P, P], F32)
-        vsc_pool = sbuf("vsc_pool", [P, POOL_PAGES * DV], U8, "value_scales")
+        vsc_pool = sbuf("vsc_pool", [P, POOL_PAGES * DV], U8)
 
         def clear(words):
             last = words.shape[1] - 1
             nc.vector.memset(words[:, 0:last], 0)
             nc.vector.memset(words[:, last:], 0)
 
-        nc.gpsimd.memset(kb_pool[:], 0.0)
+        nc.gpsimd.memset(vs_pool[:], 0.0)
         make_identity(nc, ident[:])
         clear(ks_pool[0:rows_at, :].bitcast(I32))
         clear(vsc_pool[:].bitcast(I32))
@@ -86,7 +84,7 @@ def tile_attend_pkv4q_soft_kb_kernel(
             vsc_pool[0:16, :].bitcast(I32).rearrange("f (u e) -> f u e", u=POOL_PAGES),
             v_scales.rearrange("u f e -> f u e").bitcast(I32),
         )
-        nc.scalar.dma_start(kb_pool[0:1, :], kb[0:1, :])
+        nc.scalar.dma_start(vs_pool[0:1, :], vs[0:1, :])
 
         ks_rows = sbuf("ks_rows", [P, N], U8)
         nc.vector.tensor_copy(ks_rows[:], ks_pool[:].indirect(offsets[:]))
@@ -107,125 +105,72 @@ def tile_attend_pkv4q_soft_kb_kernel(
                 qs[32 * quad : 32 * quad + 4, :].bitcast(I32).rearrange("f (o q) -> f o q", o=PASSES),
                 q_scales[0, :, 4 * quad : 4 * quad + 4, :].rearrange("o f q -> f o q").bitcast(I32),
             )
-        vs_pool = placed("vs_pool", [P, T], F32, vs_at)
-        nc.sync.dma_start(vs_pool[:], vs)
+        kb_pool = placed("kb_pool", [P, T], F32, kb_at)
+        nc.sync.dma_start(kb_pool[:], kb)
 
         def page_offsets(e):
             cols = PAGE // LIST_ROW
             return offsets[:, e * cols : (e + 1) * cols]
 
-        def bias_columns(e):
-            row = sbuf("kb_row%d" % e, [P, PAGE], F32)
-            nc.vector.tensor_copy(row[:], kb_pool[:].indirect(page_offsets(e)))
-            turned = bank(BIAS_BANK[e], "kb_turned%d" % e)
-            for j in range(TILES):
-                nc.tensor.transpose(turned[:, j * P : (j + 1) * P], row[:, j * P : (j + 1) * P], ident[:])
-            cols = sbuf("kb_cols%d" % e, [P, TILES], F32)
-            nc.scalar.activation(out=cols[:], in_=turned[:, 0:PAGE:P], func=ACT.Copy)
-            return cols
-
-        scores = [[None] * PAGES for h in range(HALVES)]
-        negated = [[None] * PAGES for h in range(HALVES)]
-        neg_max = [None] * HALVES
-
         def gather_keys(e):
-            if e == 0:
-                pairs = sbuf("k_pairs0", [P, PAGE], U32)
-                words = placed("k_parted0", [P, PASSES, PAGE], U16, kb_at)
-            else:
-                pairs = placed("k_pairs%d" % e, [P, PAGE], U32, kb_at + 4 * PAGE * e)
-                words = sbuf("k_parted%d" % e, [P, PASSES, PAGE], U16)
+            pairs = sbuf("k_pairs%d" % e, [P, PAGE], U32, "pairs%d" % e)
             nc.vector.tensor_copy(pairs[:], kw_pool[:].indirect(page_offsets(e)))
+            words = sbuf("k_parted%d" % e, [P, PASSES, PAGE], U16)
             nc.vector.tensor_copy(words[:], pairs[:].bitcast(U16).rearrange("p (n o) -> p o n", o=PASSES))
             return words
 
-        def raw_scores(e, words):
-            raws = []
-            for pair in range(TILES // 2):
-                raw = bank(2 * e + pair, "raw%d_%d" % (e, pair))
-                raws.append(raw)
-                for jj in range(2):
-                    j = 2 * pair + jj
-                    for h in range(HALVES):
-                        for o in range(PASSES):
-                            queries = slice(o * NQ + h * P, o * NQ + (h + 1) * P)
-                            lo = o * N + e * PAGE + j * P
-                            nc.tensor.matmul_mx(
-                                out=raw[:, jj * NQ + h * P : jj * NQ + (h + 1) * P],
-                                lhsT=words[:, o, j * P : (j + 1) * P].bitcast(FP4X4),
-                                lhsT_scale=k_planes[:, lo : lo + P],
-                                rhs=qw[:, queries].bitcast(FP8X4),
-                                rhs_scale=qs[:, queries],
-                                start=(o == 0),
-                                stop=(o == PASSES - 1),
-                            )
-            return raws
+        raw = [sbuf("raw%d" % h, [P, N], F32) for h in range(HALVES)]
 
-        def biased_scores(e, raws, kb_cols):
-            for h in range(HALVES):
-                scores[h][e] = bank(SCORE_BANK[e] + h, "score%d_%d" % (h, e))
-            for j in range(TILES):
-                biased = sbuf("biased%d_%d" % (e, j), [P, NQ], F32)
-                nc.scalar.activation(
-                    out=biased[:],
-                    in_=raws[j // 2][:, (j % 2) * NQ : (j % 2 + 1) * NQ],
-                    func=ACT.Identity,
-                    bias=kb_cols[:, j : j + 1],
+        def raw_scores(h, e, words):
+            acc = bank(PAGES * h + e, "raw%d_%d" % (h, e))
+            for o in range(PASSES):
+                queries = slice(o * NQ + h * P, o * NQ + (h + 1) * P)
+                lo = o * N + e * PAGE
+                nc.tensor.matmul_mx(
+                    out=acc[:],
+                    lhsT=qw[:, queries].bitcast(FP8X4),
+                    lhsT_scale=qs[:, queries],
+                    rhs=words[:, o, :].bitcast(FP4X4),
+                    rhs_scale=k_planes[:, lo : lo + PAGE],
+                    start=(o == 0),
+                    stop=(o == PASSES - 1),
                 )
-                for h in range(HALVES):
-                    nc.tensor.transpose(scores[h][e][:, j * P : (j + 1) * P], biased[:, h * P : (h + 1) * P], ident[:])
+            nc.scalar.activation(out=raw[h][:, e * PAGE : (e + 1) * PAGE], in_=acc[:], func=ACT.Copy)
 
-        def max_page(h, e):
-            negated[h][e] = placed("negated%d_%d" % (h, e), [P, PACK, P], F32, negated_at[h][e])
-            least = sbuf("neg_max%d_%d" % (h, e), [P, 1], F32, "neg_max%d_%d" % (h, e))
-            nc.vector.tensor_scalar(
-                out=negated[h][e][:],
-                in0=scores[h][e][:].rearrange("q (s r) -> q r s", r=PACK),
-                scalar1=-1.0,
-                scalar2=neg_max[h][:] if e > 0 else None,
-                op0=ALU.mult,
-                op1=ALU.min,
-                accum_out=least[:],
-            )
-            neg_max[h] = least
-
-        kb_cols = [bias_columns(e) for e in range(PAGES)]
-        vw_pool = placed("vw_pool", [P, POOL_PAGES * DV], U32, vw_at)
-        nc.sync.dma_start(
-            vw_pool[:].bitcast(I32).rearrange("p (u e) -> p u e", u=POOL_PAGES),
-            v_words.rearrange("u p e r -> p u (e r)").bitcast(I32),
-        )
-        words = [gather_keys(e) for e in range(PAGES)]
-        raws = [raw_scores(e, words[e]) for e in range(PAGES)]
         for e in range(PAGES):
-            biased_scores(e, raws[e], kb_cols[e])
-
-        vsc_rows = placed("vsc_rows", [P, PAGES * DV], U8, kb_at + 4 * PAGE)
-        nc.vector.tensor_copy(vsc_rows[:], vsc_pool[:].indirect(voffsets[:]))
-        vsc = sbuf("vsc", [P, PAGES * DV], U8, "value_scales")
-        for quad in range(QUADS):
-            nc.sync.dma_start(
-                vsc[32 * quad : 32 * quad + 4, :].bitcast(I32), vsc_rows[4 * quad : 4 * quad + 4, :].bitcast(I32)
-            )
-
-        free_at = kb_at + 4 * T
-        negated_at = [[free_at + 4 * PAGE * (PAGES * h + e) for e in range(PAGES)] for h in range(HALVES)]
-        negated_at[0][0] = vs_at
-        negated_at[1][0] = vs_at + 4 * PAGE
+            words = gather_keys(e)
+            for h in range(HALVES):
+                raw_scores(h, e, words)
 
         vs_row = sbuf("vs_row", [P, N], F32)
         nc.vector.tensor_copy(vs_row[:], vs_pool[:].indirect(offsets[:]))
         vs_cols = []
         for e in range(PAGES):
             cols = sbuf("vs_cols%d" % e, [P, PACK], F32)
-            nc.sync.dma_start(cols[:], vs_row[e : e + 1, e * PAGE : (e + 1) * PAGE])
+            nc.sync.dma_start(cols[:], vs_row[0:1, e * PAGE : (e + 1) * PAGE])
             vs_cols.append(cols)
+        vw_pool = placed("vw_pool", [P, POOL_PAGES * DV], U32, vw_at)
+        nc.sync.dma_start(
+            vw_pool[:].bitcast(I32).rearrange("p (u e) -> p u e", u=POOL_PAGES),
+            v_words.rearrange("u p e r -> p u (e r)").bitcast(I32),
+        )
 
-        for e in range(PAGES):
-            for h in range(HALVES):
-                max_page(h, e)
+        vsc_rows = sbuf("vsc_rows", [P, PAGES * DV], U8, "pairs1")
+        nc.vector.tensor_copy(vsc_rows[:], vsc_pool[:].indirect(voffsets[:]))
+        vsc = placed("vsc", [P, PAGES * DV], U8, vs_at)
+        for quad in range(QUADS):
+            nc.sync.dma_start(
+                vsc[32 * quad : 32 * quad + 4, :].bitcast(I32), vsc_rows[4 * quad : 4 * quad + 4, :].bitcast(I32)
+            )
 
-        vw = sbuf("vw", [P, PAGES * DV], U32, "neg_max0_1")
+        scores = [sbuf("scores%d" % h, [P, N], F32) for h in range(HALVES)]
+        neg_max = [sbuf("neg_max%d" % h, [P, 1], F32) for h in range(HALVES)]
+        for h in range(HALVES):
+            nc.vector.tensor_tensor(out=scores[h][:], in0=kb_pool[:].indirect(offsets[:]), in1=raw[h][:], op=ALU.add)
+        for h in range(HALVES):
+            nc.vector.tensor_reduce(out=neg_max[h][:], in_=scores[h][:], axis=AXIS.X, op=ALU.max, negate=True)
+
+        vw = sbuf("vw", [P, PAGES * DV], U32)
         nc.vector.tensor_copy(vw[:], vw_pool[:].indirect(voffsets[:]))
 
         page_sum = [sbuf("page_sum%d" % h, [P, PAGES], F32) for h in range(HALVES)]
@@ -234,10 +179,9 @@ def tile_attend_pkv4q_soft_kb_kernel(
         def weigh(h, e):
             probs = sbuf("probs%d_%d" % (h, e), [P, PACK, P], F32)
             nc.scalar.activation(
-                out=probs[:],
-                in_=negated[h][e][:],
+                out=probs[:].rearrange("q r s -> q s r"),
+                in_=scores[h][:, e * PAGE : (e + 1) * PAGE].rearrange("q (s r) -> q s r", r=PACK),
                 func=ACT.Exp,
-                scale=-1.0,
                 bias=neg_max[h][:],
                 accum_out=page_sum[h][:, e : e + 1],
             )

@@ -27,6 +27,7 @@ PASSES = D // (P * PACK)
 HALVES = NQ // P
 TILES = PAGE // P
 QUADS = 4
+BANKS = 8
 LIST_ROW = 16
 SUM_BANK = (2, 4)
 TURN_BANK = ((6, 7, 0), (1, 2, 3))
@@ -51,12 +52,11 @@ def tile_attend_pkv4q_soft_kb_kernel(
         def placed(name, shape, dtype, offset):
             return shared.tile(shape, dtype, name=name, align_bytes=64, offset=offset)
 
-        kb_at = 0
-        ks_at = kb_at + 4 * T - 64
+        vw_at = 0
+        ks_at = vw_at + 4 * POOL_PAGES * DV - 64
         qs_at = ks_at + 64 + PASSES * N
         qw_at = qs_at + PASSES * NQ
         vs_at = ks_at + 2 * T
-        vw_at = vs_at + 2 * T
         rows_at = 96
         offsets = keep.tile([P, N // LIST_ROW], U16, name="offsets")
         voffsets = keep.tile([P, PAGES * DV // LIST_ROW], U16, name="voffsets")
@@ -71,20 +71,35 @@ def tile_attend_pkv4q_soft_kb_kernel(
             nc.vector.memset(words[:, 0:last], 0)
             nc.vector.memset(words[:, last:], 0)
 
-        nc.gpsimd.memset(vs_pool[:], 0.0)
         make_identity(nc, ident[:])
+        nc.gpsimd.memset(vs_pool[:, 0 : 2 * P], 0.0)
+        nc.gpsimd.memset(vs_pool[:, 2 * P : T], 0.0)
         clear(ks_pool[0:rows_at, :].bitcast(I32))
         clear(vsc_pool[:].bitcast(I32))
 
         nc.sync.dma_start(offsets[:], offs)
         nc.sync.dma_start(ks_pool[rows_at:P, :].bitcast(I32), k_scales.rearrange("o f t -> f o t").bitcast(I32))
+        kb_rows = sbuf("kb_rows", [P, P], F32)
+        nc.sync.dma_start(kb_rows[:], kb[0 : P * P // T, :].rearrange("a (c p) -> (a c) p", p=P))
         nc.sync.dma_start(kw_pool[:].bitcast(I32), k_words[0].rearrange("p t b -> p (t b)").bitcast(I32))
         nc.sync.dma_start(voffsets[:], voffs)
         nc.sync.dma_start(
             vsc_pool[0:16, :].bitcast(I32).rearrange("f (u e) -> f u e", u=POOL_PAGES),
             v_scales.rearrange("u f e -> f u e").bitcast(I32),
         )
-        nc.scalar.dma_start(vs_pool[0:1, :], vs[0:1, :])
+        nc.sync.dma_start(vs_pool[0:1, :], vs[0:1, :])
+
+        kb_turned = bank(BANKS - 1, "kb_turned")
+        nc.tensor.transpose(kb_turned[:, 0:P], kb_rows[:], ident[:])
+        kb_cols = sbuf("kb_cols", [P, T // P], F32)
+        nc.scalar.activation(out=kb_cols[:], in_=kb_turned[:, 0 : T // P], func=ACT.Copy)
+        kb_pool = sbuf("kb_pool", [P, T], F32)
+        for u in range(POOL_PAGES):
+            spread = bank(u, "kb_spread%d" % u)
+            for j in range(TILES):
+                c = u * TILES + j
+                nc.tensor.transpose(spread[:, j * P : (j + 1) * P], kb_cols[:, c : c + 1].to_broadcast([P, P]), ident[:])
+            nc.scalar.activation(out=kb_pool[:, u * PAGE : (u + 1) * PAGE], in_=spread[:], func=ACT.Copy)
 
         ks_rows = sbuf("ks_rows", [P, N], U8)
         nc.vector.tensor_copy(ks_rows[:], ks_pool[:].indirect(offsets[:]))
@@ -105,8 +120,12 @@ def tile_attend_pkv4q_soft_kb_kernel(
                 qs[32 * quad : 32 * quad + 4, :].bitcast(I32).rearrange("f (o q) -> f o q", o=PASSES),
                 q_scales[0, :, 4 * quad : 4 * quad + 4, :].rearrange("o f q -> f o q").bitcast(I32),
             )
-        kb_pool = placed("kb_pool", [P, T], F32, kb_at)
-        nc.sync.dma_start(kb_pool[:], kb)
+
+        vw_pool = placed("vw_pool", [P, POOL_PAGES * DV], U32, vw_at)
+        nc.sync.dma_start(
+            vw_pool[:].bitcast(I32).rearrange("p (u e) -> p u e", u=POOL_PAGES),
+            v_words.rearrange("u p e r -> p u (e r)").bitcast(I32),
+        )
 
         def page_offsets(e):
             cols = PAGE // LIST_ROW
@@ -119,7 +138,8 @@ def tile_attend_pkv4q_soft_kb_kernel(
             nc.vector.tensor_copy(words[:], pairs[:].bitcast(U16).rearrange("p (n o) -> p o n", o=PASSES))
             return words
 
-        raw = [sbuf("raw%d" % h, [P, N], F32) for h in range(HALVES)]
+        raw_at = vs_at + 4 * T
+        raw = [placed("raw%d" % h, [P, N], F32, raw_at + 4 * N * (HALVES - 1 - h)) for h in range(HALVES)]
 
         def raw_scores(h, e, words):
             acc = bank(PAGES * h + e, "raw%d_%d" % (h, e))
@@ -137,10 +157,10 @@ def tile_attend_pkv4q_soft_kb_kernel(
                 )
             nc.scalar.activation(out=raw[h][:, e * PAGE : (e + 1) * PAGE], in_=acc[:], func=ACT.Copy)
 
-        for e in range(PAGES):
-            words = gather_keys(e)
-            for h in range(HALVES):
-                raw_scores(h, e, words)
+        words = [gather_keys(e) for e in range(PAGES)]
+        for h in range(HALVES):
+            for e in range(PAGES):
+                raw_scores(h, e, words[e])
 
         vs_row = sbuf("vs_row", [P, N], F32)
         nc.vector.tensor_copy(vs_row[:], vs_pool[:].indirect(offsets[:]))
@@ -149,11 +169,6 @@ def tile_attend_pkv4q_soft_kb_kernel(
             cols = sbuf("vs_cols%d" % e, [P, PACK], F32)
             nc.sync.dma_start(cols[:], vs_row[0:1, e * PAGE : (e + 1) * PAGE])
             vs_cols.append(cols)
-        vw_pool = placed("vw_pool", [P, POOL_PAGES * DV], U32, vw_at)
-        nc.sync.dma_start(
-            vw_pool[:].bitcast(I32).rearrange("p (u e) -> p u e", u=POOL_PAGES),
-            v_words.rearrange("u p e r -> p u (e r)").bitcast(I32),
-        )
 
         vsc_rows = sbuf("vsc_rows", [P, PAGES * DV], U8, "pairs1")
         nc.vector.tensor_copy(vsc_rows[:], vsc_pool[:].indirect(voffsets[:]))
@@ -170,7 +185,7 @@ def tile_attend_pkv4q_soft_kb_kernel(
         for h in range(HALVES):
             nc.vector.tensor_reduce(out=neg_max[h][:], in_=scores[h][:], axis=AXIS.X, op=ALU.max, negate=True)
 
-        vw = sbuf("vw", [P, PAGES * DV], U32)
+        vw = placed("vw", [P, PAGES * DV], U32, raw_at)
         nc.vector.tensor_copy(vw[:], vw_pool[:].indirect(voffsets[:]))
 
         page_sum = [sbuf("page_sum%d" % h, [P, PAGES], F32) for h in range(HALVES)]

@@ -29,7 +29,7 @@ TILES = PAGE // P
 QUADS = 4
 BANKS = 8
 LIST_ROW = 16
-SUM_BANK = (2, 4)
+SUM_BANK = (1, 4)
 TURN_BANK = ((6, 7, 0), (1, 2, 3))
 
 
@@ -52,11 +52,12 @@ def tile_attend_pkv4q_soft_kb_kernel(
         def placed(name, shape, dtype, offset):
             return shared.tile(shape, dtype, name=name, align_bytes=64, offset=offset)
 
-        vw_at = 0
-        ks_at = vw_at + 4 * POOL_PAGES * DV - 64
-        qs_at = ks_at + 64 + PASSES * N
-        qw_at = qs_at + PASSES * NQ
-        vs_at = ks_at + 2 * T
+        ks_at = 0
+        qs_at = ks_at + PASSES * N
+        vsc_at = qs_at + PASSES * NQ
+        vs_at = ks_at + 4 * T
+        vw_at = vs_at + 2 * T
+        scores_at = (vs_at + 2 * PAGE, vs_at + 64 - 4 * N)
         rows_at = 96
         offsets = keep.tile([P, N // LIST_ROW], U16, name="offsets")
         voffsets = keep.tile([P, PAGES * DV // LIST_ROW], U16, name="voffsets")
@@ -64,7 +65,8 @@ def tile_attend_pkv4q_soft_kb_kernel(
         ks_pool = placed("ks_pool", [P, T], U8, ks_at)
         vs_pool = placed("vs_pool", [P, T], F32, vs_at)
         ident = sbuf("ident", [P, P], F32)
-        vsc_pool = sbuf("vsc_pool", [P, POOL_PAGES * DV], U8)
+        kb_rows = sbuf("kb_rows", [P, P], F32)
+        qw = sbuf("qw", [P, PASSES * NQ], U32)
 
         def clear(words):
             last = words.shape[1] - 1
@@ -75,19 +77,16 @@ def tile_attend_pkv4q_soft_kb_kernel(
         nc.gpsimd.memset(vs_pool[:, 0 : 2 * P], 0.0)
         nc.gpsimd.memset(vs_pool[:, 2 * P : T], 0.0)
         clear(ks_pool[0:rows_at, :].bitcast(I32))
-        clear(vsc_pool[:].bitcast(I32))
 
         nc.sync.dma_start(offsets[:], offs)
         nc.sync.dma_start(ks_pool[rows_at:P, :].bitcast(I32), k_scales.rearrange("o f t -> f o t").bitcast(I32))
-        kb_rows = sbuf("kb_rows", [P, P], F32)
         nc.sync.dma_start(kb_rows[:], kb[0 : P * P // T, :].rearrange("a (c p) -> (a c) p", p=P))
-        nc.sync.dma_start(kw_pool[:].bitcast(I32), k_words[0].rearrange("p t b -> p (t b)").bitcast(I32))
         nc.sync.dma_start(voffsets[:], voffs)
+        nc.sync.dma_start(kw_pool[:].bitcast(I32), k_words[0].rearrange("p t b -> p (t b)").bitcast(I32))
         nc.sync.dma_start(
-            vsc_pool[0:16, :].bitcast(I32).rearrange("f (u e) -> f u e", u=POOL_PAGES),
-            v_scales.rearrange("u f e -> f u e").bitcast(I32),
+            qw[:].bitcast(I32).rearrange("p (o q) -> p o q", o=PASSES),
+            q_words[0].rearrange("o p q r -> p o (q r)").bitcast(I32),
         )
-        nc.sync.dma_start(vs_pool[0:1, :], vs[0:1, :])
 
         kb_turned = bank(BANKS - 1, "kb_turned")
         nc.tensor.transpose(kb_turned[:, 0:P], kb_rows[:], ident[:])
@@ -103,29 +102,25 @@ def tile_attend_pkv4q_soft_kb_kernel(
 
         ks_rows = sbuf("ks_rows", [P, N], U8)
         nc.vector.tensor_copy(ks_rows[:], ks_pool[:].indirect(offsets[:]))
-        k_planes = placed("k_planes", [P, PASSES * N], U8, ks_at + 64)
+        k_planes = placed("k_planes", [P, PASSES * N], U8, ks_at)
         for quad in range(QUADS):
             nc.sync.dma_start(
                 k_planes[32 * quad : 32 * quad + 4, :].bitcast(I32).rearrange("f (o n) -> f o n", o=PASSES),
                 ks_rows[rows_at + 8 * quad : rows_at + 8 * quad + 8, :].bitcast(I32),
             )
-        qw = placed("qw", [P, PASSES * NQ], U32, qw_at)
-        nc.sync.dma_start(
-            qw[:].bitcast(I32).rearrange("p (o q) -> p o q", o=PASSES),
-            q_words[0].rearrange("o p q r -> p o (q r)").bitcast(I32),
-        )
         qs = placed("qs", [P, PASSES * NQ], U8, qs_at)
         for quad in range(QUADS):
             nc.sync.dma_start(
                 qs[32 * quad : 32 * quad + 4, :].bitcast(I32).rearrange("f (o q) -> f o q", o=PASSES),
                 q_scales[0, :, 4 * quad : 4 * quad + 4, :].rearrange("o f q -> f o q").bitcast(I32),
             )
-
-        vw_pool = placed("vw_pool", [P, POOL_PAGES * DV], U32, vw_at)
+        vsc_pool = placed("vsc_pool", [P, POOL_PAGES * DV], U8, vsc_at)
+        clear(vsc_pool[:].bitcast(I32))
         nc.sync.dma_start(
-            vw_pool[:].bitcast(I32).rearrange("p (u e) -> p u e", u=POOL_PAGES),
-            v_words.rearrange("u p e r -> p u (e r)").bitcast(I32),
+            vsc_pool[0:16, :].bitcast(I32).rearrange("f (u e) -> f u e", u=POOL_PAGES),
+            v_scales.rearrange("u f e -> f u e").bitcast(I32),
         )
+        nc.sync.dma_start(vs_pool[0:1, :], vs[0:1, :])
 
         def page_offsets(e):
             cols = PAGE // LIST_ROW
@@ -169,16 +164,21 @@ def tile_attend_pkv4q_soft_kb_kernel(
             cols = sbuf("vs_cols%d" % e, [P, PACK], F32)
             nc.sync.dma_start(cols[:], vs_row[0:1, e * PAGE : (e + 1) * PAGE])
             vs_cols.append(cols)
+        vw_pool = placed("vw_pool", [P, POOL_PAGES * DV], U32, vw_at)
+        nc.sync.dma_start(
+            vw_pool[:].bitcast(I32).rearrange("p (u e) -> p u e", u=POOL_PAGES),
+            v_words.rearrange("u p e r -> p u (e r)").bitcast(I32),
+        )
 
         vsc_rows = sbuf("vsc_rows", [P, PAGES * DV], U8, "pairs1")
         nc.vector.tensor_copy(vsc_rows[:], vsc_pool[:].indirect(voffsets[:]))
-        vsc = placed("vsc", [P, PAGES * DV], U8, vs_at)
+        vsc = placed("vsc", [P, PAGES * DV], U8, vs_at + 64)
         for quad in range(QUADS):
             nc.sync.dma_start(
                 vsc[32 * quad : 32 * quad + 4, :].bitcast(I32), vsc_rows[4 * quad : 4 * quad + 4, :].bitcast(I32)
             )
 
-        scores = [sbuf("scores%d" % h, [P, N], F32) for h in range(HALVES)]
+        scores = [placed("scores%d" % h, [P, N], F32, scores_at[h]) for h in range(HALVES)]
         neg_max = [sbuf("neg_max%d" % h, [P, 1], F32) for h in range(HALVES)]
         for h in range(HALVES):
             nc.vector.tensor_tensor(out=scores[h][:], in0=kb_pool[:].indirect(offsets[:]), in1=raw[h][:], op=ALU.add)

@@ -25,10 +25,11 @@ PAGES = N // PAGE
 POOL_PAGES = T // PAGE
 PASSES = D // (P * PACK)
 HALVES = NQ // P
-TILES = PAGE // P
 QUADS = 4
 BANKS = 8
 LIST_ROW = 16
+RUN = T // P
+ALIGN = 64
 SUM_BANK = (1, 4)
 TURN_BANK = ((6, 7, 0), (1, 2, 3))
 
@@ -40,33 +41,35 @@ def tile_attend_pkv4q_soft_kb_kernel(
     with ExitStack() as ctx:
         keep = ctx.enter_context(tc.tile_pool(name="keep", bufs=1))
         psum = ctx.enter_context(tc.psum_pool(name="psum", bufs=1))
+        shared = ctx.enter_context(tc.tile_pool(name="shared", bufs=1))
 
-        def sbuf(name, shape, dtype, tag=""):
-            return keep.tile(shape, dtype, name=name, tag=tag, align_bytes=64)
+        def sbuf(name, shape, dtype):
+            return keep.tile(shape, dtype, name=name, align_bytes=ALIGN)
 
         def bank(index, name):
             return psum.tile([P, PAGE], F32, name=name, tag="bank%d" % index)
 
-        shared = ctx.enter_context(tc.tile_pool(name="shared", bufs=1))
-
         def placed(name, shape, dtype, offset):
-            return shared.tile(shape, dtype, name=name, align_bytes=64, offset=offset)
+            return shared.tile(shape, dtype, name=name, align_bytes=ALIGN, offset=offset)
 
-        ks_at = 0
-        qs_at = ks_at + PASSES * N
-        vsc_at = qs_at + PASSES * NQ
-        vs_at = ks_at + 4 * T
-        vw_at = vs_at + 2 * T
-        scores_at = (vs_at + 2 * PAGE, vs_at + 64 - 4 * N)
-        rows_at = 96
+        qw_at = 0
+        ks_at = qw_at + 4 * PASSES * NQ - ALIGN
+        planes_at = ks_at + ALIGN
+        vsc_at = planes_at + PASSES * N
+        rows_at = vsc_at + POOL_PAGES * DV
+        kb_at = rows_at + 4 * POOL_PAGES * DV
+        bias_at = kb_at + 4 * T
+        vs_at = bias_at + 4 * N + 4 * PAGES * DV
+        first_row = P - PASSES * LIST_ROW
+
         offsets = keep.tile([P, N // LIST_ROW], U16, name="offsets")
         voffsets = keep.tile([P, PAGES * DV // LIST_ROW], U16, name="voffsets")
         kw_pool = sbuf("kw_pool", [P, T], U32)
         ks_pool = placed("ks_pool", [P, T], U8, ks_at)
         vs_pool = placed("vs_pool", [P, T], F32, vs_at)
         ident = sbuf("ident", [P, P], F32)
-        kb_rows = sbuf("kb_rows", [P, P], F32)
-        qw = sbuf("qw", [P, PASSES * NQ], U32)
+        kb_cols = sbuf("kb_cols", [P, RUN], F32)
+        qs = sbuf("qs", [P, PASSES * NQ], U8)
 
         def clear(words):
             last = words.shape[1] - 1
@@ -74,69 +77,95 @@ def tile_attend_pkv4q_soft_kb_kernel(
             nc.vector.memset(words[:, last:], 0)
 
         make_identity(nc, ident[:])
-        nc.gpsimd.memset(vs_pool[:, 0 : 2 * P], 0.0)
-        nc.gpsimd.memset(vs_pool[:, 2 * P : T], 0.0)
-        clear(ks_pool[0:rows_at, :].bitcast(I32))
+        nc.gpsimd.memset(qs[:].bitcast(I32), 0)
+        nc.gpsimd.memset(vs_pool[:], 0.0)
+        clear(ks_pool[0:first_row, :].bitcast(I32))
 
         nc.sync.dma_start(offsets[:], offs)
-        nc.sync.dma_start(ks_pool[rows_at:P, :].bitcast(I32), k_scales.rearrange("o f t -> f o t").bitcast(I32))
-        nc.sync.dma_start(kb_rows[:], kb[0 : P * P // T, :].rearrange("a (c p) -> (a c) p", p=P))
+        nc.sync.dma_start(ks_pool[first_row:P, :].bitcast(I32), k_scales.rearrange("o f t -> f o t").bitcast(I32))
+        nc.sync.dma_start(kb_cols[:], kb[0:1, :].rearrange("a (p c) -> (a p) c", p=P))
         nc.sync.dma_start(voffsets[:], voffs)
         nc.sync.dma_start(kw_pool[:].bitcast(I32), k_words[0].rearrange("p t b -> p (t b)").bitcast(I32))
-        nc.sync.dma_start(
-            qw[:].bitcast(I32).rearrange("p (o q) -> p o q", o=PASSES),
-            q_words[0].rearrange("o p q r -> p o (q r)").bitcast(I32),
-        )
-
-        kb_turned = bank(BANKS - 1, "kb_turned")
-        nc.tensor.transpose(kb_turned[:, 0:P], kb_rows[:], ident[:])
-        kb_cols = sbuf("kb_cols", [P, T // P], F32)
-        nc.scalar.activation(out=kb_cols[:], in_=kb_turned[:, 0 : T // P], func=ACT.Copy)
-        kb_pool = sbuf("kb_pool", [P, T], F32)
-        for u in range(POOL_PAGES):
-            spread = bank(u, "kb_spread%d" % u)
-            for j in range(TILES):
-                c = u * TILES + j
-                nc.tensor.transpose(spread[:, j * P : (j + 1) * P], kb_cols[:, c : c + 1].to_broadcast([P, P]), ident[:])
-            nc.scalar.activation(out=kb_pool[:, u * PAGE : (u + 1) * PAGE], in_=spread[:], func=ACT.Copy)
-
-        ks_rows = sbuf("ks_rows", [P, N], U8)
-        nc.vector.tensor_copy(ks_rows[:], ks_pool[:].indirect(offsets[:]))
-        k_planes = placed("k_planes", [P, PASSES * N], U8, ks_at)
-        for quad in range(QUADS):
-            nc.sync.dma_start(
-                k_planes[32 * quad : 32 * quad + 4, :].bitcast(I32).rearrange("f (o n) -> f o n", o=PASSES),
-                ks_rows[rows_at + 8 * quad : rows_at + 8 * quad + 8, :].bitcast(I32),
-            )
-        qs = placed("qs", [P, PASSES * NQ], U8, qs_at)
         for quad in range(QUADS):
             nc.sync.dma_start(
                 qs[32 * quad : 32 * quad + 4, :].bitcast(I32).rearrange("f (o q) -> f o q", o=PASSES),
                 q_scales[0, :, 4 * quad : 4 * quad + 4, :].rearrange("o f q -> f o q").bitcast(I32),
             )
-        vsc_pool = placed("vsc_pool", [P, POOL_PAGES * DV], U8, vsc_at)
-        clear(vsc_pool[:].bitcast(I32))
+
+        kb_pool = placed("kb_pool", [P, T], F32, kb_at)
+        kb_runs = kb_pool[:].rearrange("p (t c) -> p t c", c=RUN)
+        for u in range(BANKS):
+            spread = bank(u, "kb_spread%d" % u)
+            for j in range(PACK):
+                c = u * PACK + j
+                nc.tensor.transpose(spread[:, j * P : (j + 1) * P], kb_cols[:, c : c + 1].to_broadcast([P, P]), ident[:])
+            nc.scalar.activation(
+                out=kb_runs[:, :, u * PACK : (u + 1) * PACK],
+                in_=spread[:].rearrange("p (j t) -> p t j", j=PACK),
+                func=ACT.Copy,
+            )
+
+        ks_rows = placed("ks_rows", [P, N], U8, rows_at)
+        nc.vector.tensor_copy(ks_rows[:], ks_pool[:].indirect(offsets[:]))
+        k_planes = placed("k_planes", [P, PASSES * N], U8, planes_at)
+        for quad in range(QUADS):
+            nc.sync.dma_start(
+                k_planes[32 * quad : 32 * quad + 4, :].bitcast(I32).rearrange("f (o n) -> f o n", o=PASSES),
+                ks_rows[first_row + 8 * quad : first_row + 8 * quad + 8, :].bitcast(I32),
+            )
+        qw = placed("qw", [P, PASSES * NQ], U32, qw_at)
         nc.sync.dma_start(
-            vsc_pool[0:16, :].bitcast(I32).rearrange("f (u e) -> f u e", u=POOL_PAGES),
-            v_scales.rearrange("u f e -> f u e").bitcast(I32),
+            qw[:].bitcast(I32).rearrange("p (o q) -> p o q", o=PASSES),
+            q_words[0].rearrange("o p q r -> p o (q r)").bitcast(I32),
         )
         nc.sync.dma_start(vs_pool[0:1, :], vs[0:1, :])
+        vsc_pool = placed("vsc_pool", [P, POOL_PAGES * DV], U8, vsc_at)
+        clear(vsc_pool[:].bitcast(I32))
+        for quad in range(QUADS):
+            nc.sync.dma_start(
+                vsc_pool[32 * quad : 32 * quad + 4, :].bitcast(I32).rearrange("f (u e) -> f u e", u=POOL_PAGES),
+                v_scales[:, 4 * quad : 4 * quad + 4, :].rearrange("u f e -> f u e").bitcast(I32),
+            )
+        vw_pool = placed("vw_pool", [P, POOL_PAGES * DV], U32, rows_at)
+        nc.sync.dma_start(
+            vw_pool[:].bitcast(I32).rearrange("p (u e) -> p u e", u=POOL_PAGES),
+            v_words.rearrange("u p e r -> p u (e r)").bitcast(I32),
+        )
 
         def page_offsets(e):
             cols = PAGE // LIST_ROW
             return offsets[:, e * cols : (e + 1) * cols]
 
+        bias_place = (1, 2, 0)
+        bias = []
+        for e in range(PAGES):
+            row = placed("bias%d" % e, [P, PAGE], F32, bias_at + 4 * PAGE * bias_place[e])
+            nc.scalar.activation(out=row[:], in_=kb_pool[:].indirect(page_offsets(e)), func=ACT.Copy)
+            bias.append(row)
+        vs_row = placed("vs_row", [P, N], F32, kb_at)
+        nc.scalar.activation(out=vs_row[:], in_=vs_pool[:].indirect(offsets[:]), func=ACT.Copy)
+        vs_cols = []
+        for e in range(PAGES):
+            cols = sbuf("vs_cols%d" % e, [P, PACK], F32)
+            nc.sync.dma_start(cols[:], vs_row[0:1, e * PAGE : (e + 1) * PAGE])
+            vs_cols.append(cols)
+
         def gather_keys(e):
-            pairs = sbuf("k_pairs%d" % e, [P, PAGE], U32, "pairs%d" % e)
+            pairs = sbuf("k_pairs%d" % e, [P, PAGE], U32)
             nc.vector.tensor_copy(pairs[:], kw_pool[:].indirect(page_offsets(e)))
             words = sbuf("k_parted%d" % e, [P, PASSES, PAGE], U16)
             nc.vector.tensor_copy(words[:], pairs[:].bitcast(U16).rearrange("p (n o) -> p o n", o=PASSES))
             return words
 
-        raw_at = vs_at + 4 * T
-        raw = [placed("raw%d" % h, [P, N], F32, raw_at + 4 * N * (HALVES - 1 - h)) for h in range(HALVES)]
+        words = [gather_keys(e) for e in range(PAGES)]
 
-        def raw_scores(h, e, words):
+        vsc = sbuf("vsc", [P, PAGES * DV], U8)
+        nc.vector.tensor_copy(vsc[:], vsc_pool[:].indirect(voffsets[:]))
+
+        scores = [sbuf("scores%d" % h, [P, N], F32) for h in range(HALVES)]
+        neg_max = [sbuf("neg_max%d" % h, [P, 1], F32) for h in range(HALVES)]
+
+        def score(h, e):
             acc = bank(PAGES * h + e, "raw%d_%d" % (h, e))
             for o in range(PASSES):
                 queries = slice(o * NQ + h * P, o * NQ + (h + 1) * P)
@@ -145,54 +174,28 @@ def tile_attend_pkv4q_soft_kb_kernel(
                     out=acc[:],
                     lhsT=qw[:, queries].bitcast(FP8X4),
                     lhsT_scale=qs[:, queries],
-                    rhs=words[:, o, :].bitcast(FP4X4),
+                    rhs=words[e][:, o, :].bitcast(FP4X4),
                     rhs_scale=k_planes[:, lo : lo + PAGE],
                     start=(o == 0),
                     stop=(o == PASSES - 1),
                 )
-            nc.scalar.activation(out=raw[h][:, e * PAGE : (e + 1) * PAGE], in_=acc[:], func=ACT.Copy)
-
-        words = [gather_keys(e) for e in range(PAGES)]
-        for h in range(HALVES):
-            for e in range(PAGES):
-                raw_scores(h, e, words[e])
-
-        vs_row = sbuf("vs_row", [P, N], F32)
-        nc.vector.tensor_copy(vs_row[:], vs_pool[:].indirect(offsets[:]))
-        vs_cols = []
-        for e in range(PAGES):
-            cols = sbuf("vs_cols%d" % e, [P, PACK], F32)
-            nc.sync.dma_start(cols[:], vs_row[0:1, e * PAGE : (e + 1) * PAGE])
-            vs_cols.append(cols)
-        vw_pool = placed("vw_pool", [P, POOL_PAGES * DV], U32, vw_at)
-        nc.sync.dma_start(
-            vw_pool[:].bitcast(I32).rearrange("p (u e) -> p u e", u=POOL_PAGES),
-            v_words.rearrange("u p e r -> p u (e r)").bitcast(I32),
-        )
-
-        vsc_rows = sbuf("vsc_rows", [P, PAGES * DV], U8, "pairs1")
-        nc.vector.tensor_copy(vsc_rows[:], vsc_pool[:].indirect(voffsets[:]))
-        vsc = placed("vsc", [P, PAGES * DV], U8, vs_at + 64)
-        for quad in range(QUADS):
-            nc.sync.dma_start(
-                vsc[32 * quad : 32 * quad + 4, :].bitcast(I32), vsc_rows[4 * quad : 4 * quad + 4, :].bitcast(I32)
+            nc.vector.tensor_tensor(
+                out=scores[h][:, e * PAGE : (e + 1) * PAGE], in0=acc[:], in1=bias[e][:], op=ALU.add
             )
 
-        scores = [placed("scores%d" % h, [P, N], F32, scores_at[h]) for h in range(HALVES)]
-        neg_max = [sbuf("neg_max%d" % h, [P, 1], F32) for h in range(HALVES)]
         for h in range(HALVES):
-            nc.vector.tensor_tensor(out=scores[h][:], in0=kb_pool[:].indirect(offsets[:]), in1=raw[h][:], op=ALU.add)
-        for h in range(HALVES):
+            for e in range(PAGES):
+                score(h, e)
             nc.vector.tensor_reduce(out=neg_max[h][:], in_=scores[h][:], axis=AXIS.X, op=ALU.max, negate=True)
 
-        vw = placed("vw", [P, PAGES * DV], U32, raw_at)
+        vw = placed("vw", [P, PAGES * DV], U32, bias_at + 4 * PAGE * bias_place[1])
         nc.vector.tensor_copy(vw[:], vw_pool[:].indirect(voffsets[:]))
 
         page_sum = [sbuf("page_sum%d" % h, [P, PAGES], F32) for h in range(HALVES)]
         sums = [None] * HALVES
 
         def weigh(h, e):
-            probs = sbuf("probs%d_%d" % (h, e), [P, PACK, P], F32)
+            probs = placed("probs%d_%d" % (h, e), [P, PACK, P], F32, vs_at + 4 * PAGE * (PAGES * h + e))
             nc.scalar.activation(
                 out=probs[:].rearrange("q r s -> q s r"),
                 in_=scores[h][:, e * PAGE : (e + 1) * PAGE].rearrange("q (s r) -> q s r", r=PACK),

@@ -52,14 +52,12 @@ def tile_attend_pkv4q_soft_kb_kernel(
         def placed(name, shape, dtype, offset):
             return shared.tile(shape, dtype, name=name, align_bytes=ALIGN, offset=offset)
 
-        qw_at = 0
-        ks_at = qw_at + 4 * PASSES * NQ - ALIGN
-        planes_at = ks_at + ALIGN
-        vsc_at = planes_at + PASSES * N
-        rows_at = vsc_at + POOL_PAGES * DV
+        ks_at = 0
+        rows_at = ks_at + T
         kb_at = rows_at + 4 * POOL_PAGES * DV
         bias_at = kb_at + 4 * T
         vs_at = bias_at + 4 * N + 4 * PAGES * DV
+        span = N + NQ
         first_row = P - PASSES * LIST_ROW
 
         offsets = keep.tile([P, N // LIST_ROW], U16, name="offsets")
@@ -69,7 +67,9 @@ def tile_attend_pkv4q_soft_kb_kernel(
         vs_pool = placed("vs_pool", [P, T], F32, vs_at)
         ident = sbuf("ident", [P, P], F32)
         kb_cols = sbuf("kb_cols", [P, RUN], F32)
-        qs = sbuf("qs", [P, PASSES * NQ], U8)
+        qw = sbuf("qw", [P, PASSES * NQ], U32)
+        vsc_pool = sbuf("vsc_pool", [P, POOL_PAGES * DV], U8)
+        scale_rows = placed("scale_rows", [P, span], U8, rows_at)
 
         def clear(words):
             last = words.shape[1] - 1
@@ -77,20 +77,23 @@ def tile_attend_pkv4q_soft_kb_kernel(
             nc.vector.memset(words[:, last:], 0)
 
         make_identity(nc, ident[:])
-        nc.gpsimd.memset(qs[:].bitcast(I32), 0)
-        nc.gpsimd.memset(vs_pool[:], 0.0)
+        nc.gpsimd.memset(vs_pool[:, 0 : 2 * P], 0.0)
+        nc.gpsimd.memset(vs_pool[:, 2 * P : T], 0.0)
+        nc.gpsimd.memset(vsc_pool[:].bitcast(I32), 0)
         clear(ks_pool[0:first_row, :].bitcast(I32))
 
         nc.sync.dma_start(offsets[:], offs)
         nc.sync.dma_start(ks_pool[first_row:P, :].bitcast(I32), k_scales.rearrange("o f t -> f o t").bitcast(I32))
         nc.sync.dma_start(kb_cols[:], kb[0:1, :].rearrange("a (p c) -> (a p) c", p=P))
-        nc.sync.dma_start(voffsets[:], voffs)
+        nc.sync.dma_start(
+            scale_rows[first_row:P, N:span].bitcast(I32), q_scales[0].rearrange("o f q -> f o q").bitcast(I32)
+        )
         nc.sync.dma_start(kw_pool[:].bitcast(I32), k_words[0].rearrange("p t b -> p (t b)").bitcast(I32))
-        for quad in range(QUADS):
-            nc.sync.dma_start(
-                qs[32 * quad : 32 * quad + 4, :].bitcast(I32).rearrange("f (o q) -> f o q", o=PASSES),
-                q_scales[0, :, 4 * quad : 4 * quad + 4, :].rearrange("o f q -> f o q").bitcast(I32),
-            )
+        nc.sync.dma_start(
+            qw[:].bitcast(I32).rearrange("p (o q) -> p o q", o=PASSES),
+            q_words[0].rearrange("o p q r -> p o (q r)").bitcast(I32),
+        )
+        nc.sync.dma_start(voffsets[:], voffs)
 
         kb_pool = placed("kb_pool", [P, T], F32, kb_at)
         kb_runs = kb_pool[:].rearrange("p (t c) -> p t c", c=RUN)
@@ -105,22 +108,16 @@ def tile_attend_pkv4q_soft_kb_kernel(
                 func=ACT.Copy,
             )
 
-        ks_rows = placed("ks_rows", [P, N], U8, rows_at)
+        ks_rows = sbuf("ks_rows", [P, N], U8)
         nc.vector.tensor_copy(ks_rows[:], ks_pool[:].indirect(offsets[:]))
-        k_planes = placed("k_planes", [P, PASSES * N], U8, planes_at)
+        nc.vector.tensor_copy(scale_rows[first_row:P, 0:N].bitcast(I32), ks_rows[first_row:P, :].bitcast(I32))
+        planes = placed("planes", [P, PASSES * span], U8, ks_at)
         for quad in range(QUADS):
             nc.sync.dma_start(
-                k_planes[32 * quad : 32 * quad + 4, :].bitcast(I32).rearrange("f (o n) -> f o n", o=PASSES),
-                ks_rows[first_row + 8 * quad : first_row + 8 * quad + 8, :].bitcast(I32),
+                planes[32 * quad : 32 * quad + 4, :].bitcast(I32).rearrange("f (o n) -> f o n", o=PASSES),
+                scale_rows[first_row + 8 * quad : first_row + 8 * quad + 8, :].bitcast(I32),
             )
-        qw = placed("qw", [P, PASSES * NQ], U32, qw_at)
-        nc.sync.dma_start(
-            qw[:].bitcast(I32).rearrange("p (o q) -> p o q", o=PASSES),
-            q_words[0].rearrange("o p q r -> p o (q r)").bitcast(I32),
-        )
         nc.sync.dma_start(vs_pool[0:1, :], vs[0:1, :])
-        vsc_pool = placed("vsc_pool", [P, POOL_PAGES * DV], U8, vsc_at)
-        clear(vsc_pool[:].bitcast(I32))
         for quad in range(QUADS):
             nc.sync.dma_start(
                 vsc_pool[32 * quad : 32 * quad + 4, :].bitcast(I32).rearrange("f (u e) -> f u e", u=POOL_PAGES),
@@ -142,13 +139,6 @@ def tile_attend_pkv4q_soft_kb_kernel(
             row = placed("bias%d" % e, [P, PAGE], F32, bias_at + 4 * PAGE * bias_place[e])
             nc.scalar.activation(out=row[:], in_=kb_pool[:].indirect(page_offsets(e)), func=ACT.Copy)
             bias.append(row)
-        vs_row = placed("vs_row", [P, N], F32, kb_at)
-        nc.scalar.activation(out=vs_row[:], in_=vs_pool[:].indirect(offsets[:]), func=ACT.Copy)
-        vs_cols = []
-        for e in range(PAGES):
-            cols = sbuf("vs_cols%d" % e, [P, PACK], F32)
-            nc.sync.dma_start(cols[:], vs_row[0:1, e * PAGE : (e + 1) * PAGE])
-            vs_cols.append(cols)
 
         def gather_keys(e):
             pairs = sbuf("k_pairs%d" % e, [P, PAGE], U32)
@@ -159,23 +149,32 @@ def tile_attend_pkv4q_soft_kb_kernel(
 
         words = [gather_keys(e) for e in range(PAGES)]
 
+        vs_row = sbuf("vs_row", [P, N], F32)
+        nc.vector.tensor_copy(vs_row[:], vs_pool[:].indirect(offsets[:]))
+        vs_cols = []
+        for e in range(PAGES):
+            cols = sbuf("vs_cols%d" % e, [P, PACK], F32)
+            nc.sync.dma_start(cols[:], vs_row[0:1, e * PAGE : (e + 1) * PAGE])
+            vs_cols.append(cols)
+
         vsc = sbuf("vsc", [P, PAGES * DV], U8)
         nc.vector.tensor_copy(vsc[:], vsc_pool[:].indirect(voffsets[:]))
 
-        scores = [sbuf("scores%d" % h, [P, N], F32) for h in range(HALVES)]
+        scores = [placed("scores%d" % h, [P, N], F32, vs_at + 4 * N * h) for h in range(HALVES)]
         neg_max = [sbuf("neg_max%d" % h, [P, 1], F32) for h in range(HALVES)]
 
         def score(h, e):
             acc = bank(PAGES * h + e, "raw%d_%d" % (h, e))
             for o in range(PASSES):
                 queries = slice(o * NQ + h * P, o * NQ + (h + 1) * P)
-                lo = o * N + e * PAGE
+                lo = o * span + e * PAGE
+                q_lo = o * span + N + h * P
                 nc.tensor.matmul_mx(
                     out=acc[:],
                     lhsT=qw[:, queries].bitcast(FP8X4),
-                    lhsT_scale=qs[:, queries],
+                    lhsT_scale=planes[:, q_lo : q_lo + P],
                     rhs=words[e][:, o, :].bitcast(FP4X4),
-                    rhs_scale=k_planes[:, lo : lo + PAGE],
+                    rhs_scale=planes[:, lo : lo + PAGE],
                     start=(o == 0),
                     stop=(o == PASSES - 1),
                 )
@@ -195,7 +194,7 @@ def tile_attend_pkv4q_soft_kb_kernel(
         sums = [None] * HALVES
 
         def weigh(h, e):
-            probs = placed("probs%d_%d" % (h, e), [P, PACK, P], F32, vs_at + 4 * PAGE * (PAGES * h + e))
+            probs = sbuf("probs%d_%d" % (h, e), [P, PACK, P], F32)
             nc.scalar.activation(
                 out=probs[:].rearrange("q r s -> q s r"),
                 in_=scores[h][:, e * PAGE : (e + 1) * PAGE].rearrange("q (s r) -> q s r", r=PACK),

@@ -53,7 +53,8 @@ def tile_attend_pkv4q_soft_kb_kernel(
             return shared.tile(shape, dtype, name=name, align_bytes=ALIGN, offset=offset)
 
         ks_at = 0
-        rows_at = ks_at + T
+        vsc_at = ks_at + PASSES * (N + NQ)
+        rows_at = vsc_at + POOL_PAGES * DV
         kb_at = rows_at + 4 * POOL_PAGES * DV
         bias_at = kb_at + 4 * T
         vs_at = bias_at + 4 * N + 4 * PAGES * DV
@@ -66,9 +67,8 @@ def tile_attend_pkv4q_soft_kb_kernel(
         ks_pool = placed("ks_pool", [P, T], U8, ks_at)
         vs_pool = placed("vs_pool", [P, T], F32, vs_at)
         ident = sbuf("ident", [P, P], F32)
-        kb_cols = sbuf("kb_cols", [P, RUN], F32)
+        kb_rows = sbuf("kb_rows", [P, P], F32)
         qw = sbuf("qw", [P, PASSES * NQ], U32)
-        vsc_pool = sbuf("vsc_pool", [P, POOL_PAGES * DV], U8)
         scale_rows = placed("scale_rows", [P, span], U8, rows_at)
 
         def clear(words):
@@ -79,12 +79,11 @@ def tile_attend_pkv4q_soft_kb_kernel(
         make_identity(nc, ident[:])
         nc.gpsimd.memset(vs_pool[:, 0 : 2 * P], 0.0)
         nc.gpsimd.memset(vs_pool[:, 2 * P : T], 0.0)
-        nc.gpsimd.memset(vsc_pool[:].bitcast(I32), 0)
         clear(ks_pool[0:first_row, :].bitcast(I32))
 
         nc.sync.dma_start(offsets[:], offs)
         nc.sync.dma_start(ks_pool[first_row:P, :].bitcast(I32), k_scales.rearrange("o f t -> f o t").bitcast(I32))
-        nc.sync.dma_start(kb_cols[:], kb[0:1, :].rearrange("a (p c) -> (a p) c", p=P))
+        nc.sync.dma_start(kb_rows[:], kb[0 : P * P // T, :].rearrange("a (c p) -> (a c) p", p=P))
         nc.sync.dma_start(
             scale_rows[first_row:P, N:span].bitcast(I32), q_scales[0].rearrange("o f q -> f o q").bitcast(I32)
         )
@@ -96,17 +95,16 @@ def tile_attend_pkv4q_soft_kb_kernel(
         nc.sync.dma_start(voffsets[:], voffs)
 
         kb_pool = placed("kb_pool", [P, T], F32, kb_at)
-        kb_runs = kb_pool[:].rearrange("p (t c) -> p t c", c=RUN)
+        kb_turned = bank(BANKS - 1, "kb_turned")
+        nc.tensor.transpose(kb_turned[:, 0:P], kb_rows[:], ident[:])
+        kb_cols = sbuf("kb_cols", [P, RUN], F32)
+        nc.scalar.activation(out=kb_cols[:], in_=kb_turned[:, 0:RUN], func=ACT.Copy)
         for u in range(BANKS):
             spread = bank(u, "kb_spread%d" % u)
             for j in range(PACK):
                 c = u * PACK + j
                 nc.tensor.transpose(spread[:, j * P : (j + 1) * P], kb_cols[:, c : c + 1].to_broadcast([P, P]), ident[:])
-            nc.scalar.activation(
-                out=kb_runs[:, :, u * PACK : (u + 1) * PACK],
-                in_=spread[:].rearrange("p (j t) -> p t j", j=PACK),
-                func=ACT.Copy,
-            )
+            nc.scalar.activation(out=kb_pool[:, u * PAGE : (u + 1) * PAGE], in_=spread[:], func=ACT.Copy)
 
         ks_rows = sbuf("ks_rows", [P, N], U8)
         nc.vector.tensor_copy(ks_rows[:], ks_pool[:].indirect(offsets[:]))
@@ -117,12 +115,14 @@ def tile_attend_pkv4q_soft_kb_kernel(
                 planes[32 * quad : 32 * quad + 4, :].bitcast(I32).rearrange("f (o n) -> f o n", o=PASSES),
                 scale_rows[first_row + 8 * quad : first_row + 8 * quad + 8, :].bitcast(I32),
             )
-        nc.sync.dma_start(vs_pool[0:1, :], vs[0:1, :])
+        vsc_pool = placed("vsc_pool", [P, POOL_PAGES * DV], U8, vsc_at)
+        clear(vsc_pool[:].bitcast(I32))
         for quad in range(QUADS):
             nc.sync.dma_start(
                 vsc_pool[32 * quad : 32 * quad + 4, :].bitcast(I32).rearrange("f (u e) -> f u e", u=POOL_PAGES),
                 v_scales[:, 4 * quad : 4 * quad + 4, :].rearrange("u f e -> f u e").bitcast(I32),
             )
+        nc.sync.dma_start(vs_pool[0:1, :], vs[0:1, :])
         vw_pool = placed("vw_pool", [P, POOL_PAGES * DV], U32, rows_at)
         nc.sync.dma_start(
             vw_pool[:].bitcast(I32).rearrange("p (u e) -> p u e", u=POOL_PAGES),
@@ -133,7 +133,7 @@ def tile_attend_pkv4q_soft_kb_kernel(
             cols = PAGE // LIST_ROW
             return offsets[:, e * cols : (e + 1) * cols]
 
-        bias_place = (1, 2, 0)
+        bias_place = (0, 1, 2)
         bias = []
         for e in range(PAGES):
             row = placed("bias%d" % e, [P, PAGE], F32, bias_at + 4 * PAGE * bias_place[e])
@@ -149,6 +149,8 @@ def tile_attend_pkv4q_soft_kb_kernel(
 
         words = [gather_keys(e) for e in range(PAGES)]
 
+        vsc = sbuf("vsc", [P, PAGES * DV], U8)
+        nc.vector.tensor_copy(vsc[:], vsc_pool[:].indirect(voffsets[:]))
         vs_row = sbuf("vs_row", [P, N], F32)
         nc.vector.tensor_copy(vs_row[:], vs_pool[:].indirect(offsets[:]))
         vs_cols = []
@@ -156,9 +158,6 @@ def tile_attend_pkv4q_soft_kb_kernel(
             cols = sbuf("vs_cols%d" % e, [P, PACK], F32)
             nc.sync.dma_start(cols[:], vs_row[0:1, e * PAGE : (e + 1) * PAGE])
             vs_cols.append(cols)
-
-        vsc = sbuf("vsc", [P, PAGES * DV], U8)
-        nc.vector.tensor_copy(vsc[:], vsc_pool[:].indirect(voffsets[:]))
 
         scores = [placed("scores%d" % h, [P, N], F32, vs_at + 4 * N * h) for h in range(HALVES)]
         neg_max = [sbuf("neg_max%d" % h, [P, 1], F32) for h in range(HALVES)]
@@ -182,12 +181,13 @@ def tile_attend_pkv4q_soft_kb_kernel(
                 out=scores[h][:, e * PAGE : (e + 1) * PAGE], in0=acc[:], in1=bias[e][:], op=ALU.add
             )
 
-        for h in range(HALVES):
-            for e in range(PAGES):
+        for e in range(PAGES):
+            for h in range(HALVES):
                 score(h, e)
+        for h in range(HALVES):
             nc.vector.tensor_reduce(out=neg_max[h][:], in_=scores[h][:], axis=AXIS.X, op=ALU.max, negate=True)
 
-        vw = placed("vw", [P, PAGES * DV], U32, bias_at + 4 * PAGE * bias_place[1])
+        vw = placed("vw", [P, PAGES * DV], U32, bias_at + 4 * PAGE * bias_place[2])
         nc.vector.tensor_copy(vw[:], vw_pool[:].indirect(voffsets[:]))
 
         page_sum = [sbuf("page_sum%d" % h, [P, PAGES], F32) for h in range(HALVES)]

@@ -30,6 +30,7 @@ BANKS = 8
 LIST_ROW = 16
 RUN = T // P
 ALIGN = 64
+VS_ROW = 8
 SUM_BANK = (1, 4)
 TURN_BANK = ((6, 7, 0), (1, 2, 3))
 
@@ -71,15 +72,9 @@ def tile_attend_pkv4q_soft_kb_kernel(
         qw = sbuf("qw", [P, PASSES * NQ], U32)
         scale_rows = placed("scale_rows", [P, span], U8, rows_at)
 
-        def clear(words):
-            last = words.shape[1] - 1
-            nc.vector.memset(words[:, 0:last], 0)
-            nc.vector.memset(words[:, last:], 0)
-
         make_identity(nc, ident[:])
-        nc.gpsimd.memset(vs_pool[:, 0 : 2 * P], 0.0)
-        nc.gpsimd.memset(vs_pool[:, 2 * P : T], 0.0)
-        clear(ks_pool[0:first_row, :].bitcast(I32))
+        nc.vector.memset(ks_pool[0:first_row, :].bitcast(I32), 0)
+        nc.vector.memset(vs_pool[:], 0.0)
 
         nc.sync.dma_start(offsets[:], offs)
         nc.sync.dma_start(ks_pool[first_row:P, :].bitcast(I32), k_scales.rearrange("o f t -> f o t").bitcast(I32))
@@ -116,13 +111,13 @@ def tile_attend_pkv4q_soft_kb_kernel(
                 scale_rows[first_row + 8 * quad : first_row + 8 * quad + 8, :].bitcast(I32),
             )
         vsc_pool = placed("vsc_pool", [P, POOL_PAGES * DV], U8, vsc_at)
-        clear(vsc_pool[:].bitcast(I32))
+        nc.vector.memset(vsc_pool[:].bitcast(I32), 0)
         for quad in range(QUADS):
             nc.sync.dma_start(
                 vsc_pool[32 * quad : 32 * quad + 4, :].bitcast(I32).rearrange("f (u e) -> f u e", u=POOL_PAGES),
                 v_scales[:, 4 * quad : 4 * quad + 4, :].rearrange("u f e -> f u e").bitcast(I32),
             )
-        nc.sync.dma_start(vs_pool[0:1, :], vs[0:1, :])
+        nc.sync.dma_start(vs_pool[VS_ROW : VS_ROW + 1, :], vs[0:1, :])
         vw_pool = placed("vw_pool", [P, POOL_PAGES * DV], U32, rows_at)
         nc.sync.dma_start(
             vw_pool[:].bitcast(I32).rearrange("p (u e) -> p u e", u=POOL_PAGES),
@@ -156,7 +151,7 @@ def tile_attend_pkv4q_soft_kb_kernel(
         vs_cols = []
         for e in range(PAGES):
             cols = sbuf("vs_cols%d" % e, [P, PACK], F32)
-            nc.sync.dma_start(cols[:], vs_row[0:1, e * PAGE : (e + 1) * PAGE])
+            nc.sync.dma_start(cols[:], vs_row[VS_ROW : VS_ROW + 1, e * PAGE : (e + 1) * PAGE])
             vs_cols.append(cols)
 
         scores = [placed("scores%d" % h, [P, N], F32, vs_at + 4 * N * h) for h in range(HALVES)]

from contextlib import ExitStack

import concourse.mybir as mybir
from concourse.masks import make_identity

N, T, D, DV, NQ = 1536, 4096, 1024, 256, 256
PAGE = 512
FLOPS = 2 * NQ * N * (D + DV)

F32 = mybir.dt.float32
BF16 = mybir.dt.bfloat16
I32 = mybir.dt.int32
U32 = mybir.dt.uint32
U16 = mybir.dt.uint16
U8 = mybir.dt.uint8
FP8X4 = mybir.dt.float8_e4m3fn_x4
FP4X4 = mybir.dt.float4_e2m1fn_x4
ACT = mybir.ActivationFunctionType
ALU = mybir.AluOpType
AXIS = mybir.AxisListType

P = 128
PACK = 4
PAGES = N // PAGE
POOL_PAGES = T // PAGE
PASSES = D // (P * PACK)
HALVES = NQ // P
QUADS = 4
BANKS = 8
LIST_ROW = 16
RUN = T // P
ALIGN = 64
VS_ROW = 8
SUM_BANK = (1, 4)
TURN_BANK = ((6, 7, 0), (1, 2, 3))


def tile_attend_pkv4q_soft_kb_kernel(
    tc, q_words, q_scales, k_words, k_scales, v_words, v_scales, vs, kb, offs, voffs, out
):
    nc = tc.nc
    with ExitStack() as ctx:
        keep = ctx.enter_context(tc.tile_pool(name="keep", bufs=1))
        psum = ctx.enter_context(tc.psum_pool(name="psum", bufs=1))
        shared = ctx.enter_context(tc.tile_pool(name="shared", bufs=1))

        def sbuf(name, shape, dtype):
            return keep.tile(shape, dtype, name=name, align_bytes=ALIGN)

        def bank(index, name):
            return psum.tile([P, PAGE], F32, name=name, tag="bank%d" % index)

        def placed(name, shape, dtype, offset):
            return shared.tile(shape, dtype, name=name, align_bytes=ALIGN, offset=offset)

        ks_at = 0
        vsc_at = ks_at + PASSES * (N + NQ)
        rows_at = vsc_at + POOL_PAGES * DV
        kb_at = rows_at + 4 * POOL_PAGES * DV
        bias_at = kb_at + 4 * T
        vs_at = bias_at + 4 * N + 4 * PAGES * DV
        span = N + NQ
        first_row = P - PASSES * LIST_ROW

        offsets = keep.tile([P, N // LIST_ROW], U16, name="offsets")
        voffsets = keep.tile([P, PAGES * DV // LIST_ROW], U16, name="voffsets")
        kw_pool = sbuf("kw_pool", [P, T], U32)
        ks_pool = placed("ks_pool", [P, T], U8, ks_at)
        vs_pool = placed("vs_pool", [P, T], F32, vs_at)
        ident = sbuf("ident", [P, P], F32)
        kb_rows = sbuf("kb_rows", [P, P], F32)
        qw = sbuf("qw", [P, PASSES * NQ], U32)
        scale_rows = placed("scale_rows", [P, span], U8, rows_at)

        make_identity(nc, ident[:])
        nc.vector.memset(ks_pool[0:first_row, :].bitcast(I32), 0)
        nc.vector.memset(vs_pool[:], 0.0)

        nc.sync.dma_start(offsets[:], offs)
        nc.sync.dma_start(ks_pool[first_row:P, :].bitcast(I32), k_scales.rearrange("o f t -> f o t").bitcast(I32))
        nc.sync.dma_start(kb_rows[:], kb[0 : P * P // T, :].rearrange("a (c p) -> (a c) p", p=P))
        nc.sync.dma_start(
            scale_rows[first_row:P, N:span].bitcast(I32), q_scales[0].rearrange("o f q -> f o q").bitcast(I32)
        )
        nc.sync.dma_start(kw_pool[:].bitcast(I32), k_words[0].rearrange("p t b -> p (t b)").bitcast(I32))
        nc.sync.dma_start(
            qw[:].bitcast(I32).rearrange("p (o q) -> p o q", o=PASSES),
            q_words[0].rearrange("o p q r -> p o (q r)").bitcast(I32),
        )
        nc.sync.dma_start(voffsets[:], voffs)

        kb_pool = placed("kb_pool", [P, T], F32, kb_at)
        kb_turned = bank(BANKS - 1, "kb_turned")
        nc.tensor.transpose(kb_turned[:, 0:P], kb_rows[:], ident[:])
        kb_cols = sbuf("kb_cols", [P, RUN], F32)
        nc.scalar.activation(out=kb_cols[:], in_=kb_turned[:, 0:RUN], func=ACT.Copy)
        for u in range(BANKS):
            spread = bank(u, "kb_spread%d" % u)
            for j in range(PACK):
                c = u * PACK + j
                nc.tensor.transpose(spread[:, j * P : (j + 1) * P], kb_cols[:, c : c + 1].to_broadcast([P, P]), ident[:])
            nc.scalar.activation(out=kb_pool[:, u * PAGE : (u + 1) * PAGE], in_=spread[:], func=ACT.Copy)

        ks_rows = sbuf("ks_rows", [P, N], U8)
        nc.vector.tensor_copy(ks_rows[:], ks_pool[:].indirect(offsets[:]))
        nc.vector.tensor_copy(scale_rows[first_row:P, 0:N].bitcast(I32), ks_rows[first_row:P, :].bitcast(I32))
        planes = placed("planes", [P, PASSES * span], U8, ks_at)
        for quad in range(QUADS):
            nc.sync.dma_start(
                planes[32 * quad : 32 * quad + 4, :].bitcast(I32).rearrange("f (o n) -> f o n", o=PASSES),
                scale_rows[first_row + 8 * quad : first_row + 8 * quad + 8, :].bitcast(I32),
            )
        vsc_pool = placed("vsc_pool", [P, POOL_PAGES * DV], U8, vsc_at)
        nc.vector.memset(vsc_pool[:].bitcast(I32), 0)
        for quad in range(QUADS):
            nc.sync.dma_start(
                vsc_pool[32 * quad : 32 * quad + 4, :].bitcast(I32).rearrange("f (u e) -> f u e", u=POOL_PAGES),
                v_scales[:, 4 * quad : 4 * quad + 4, :].rearrange("u f e -> f u e").bitcast(I32),
            )
        nc.sync.dma_start(vs_pool[VS_ROW : VS_ROW + 1, :], vs[0:1, :])
        vw_pool = placed("vw_pool", [P, POOL_PAGES * DV], U32, rows_at)
        nc.sync.dma_start(
            vw_pool[:].bitcast(I32).rearrange("p (u e) -> p u e", u=POOL_PAGES),
            v_words.rearrange("u p e r -> p u (e r)").bitcast(I32),
        )

        def page_offsets(e):
            cols = PAGE // LIST_ROW
            return offsets[:, e * cols : (e + 1) * cols]

        bias_place = (0, 1, 2)
        bias = []
        for e in range(PAGES):
            row = placed("bias%d" % e, [P, PAGE], F32, bias_at + 4 * PAGE * bias_place[e])
            nc.scalar.activation(out=row[:], in_=kb_pool[:].indirect(page_offsets(e)), func=ACT.Copy)
            bias.append(row)

        def gather_keys(e):
            pairs = sbuf("k_pairs%d" % e, [P, PAGE], U32)
            nc.vector.tensor_copy(pairs[:], kw_pool[:].indirect(page_offsets(e)))
            words = sbuf("k_parted%d" % e, [P, PASSES, PAGE], U16)
            nc.vector.tensor_copy(words[:], pairs[:].bitcast(U16).rearrange("p (n o) -> p o n", o=PASSES))
            return words

        words = [gather_keys(e) for e in range(PAGES)]

        vsc = sbuf("vsc", [P, PAGES * DV], U8)
        nc.vector.tensor_copy(vsc[:], vsc_pool[:].indirect(voffsets[:]))
        vs_row = sbuf("vs_row", [P, N], F32)
        nc.vector.tensor_copy(vs_row[:], vs_pool[:].indirect(offsets[:]))
        vs_cols = []
        for e in range(PAGES):
            cols = sbuf("vs_cols%d" % e, [P, PACK], F32)
            nc.sync.dma_start(cols[:], vs_row[VS_ROW : VS_ROW + 1, e * PAGE : (e + 1) * PAGE])
            vs_cols.append(cols)

        scores = [placed("scores%d" % h, [P, N], F32, vs_at + 4 * N * h) for h in range(HALVES)]
        neg_max = [sbuf("neg_max%d" % h, [P, 1], F32) for h in range(HALVES)]

        def score(h, e):
            acc = bank(PAGES * h + e, "raw%d_%d" % (h, e))
            for o in range(PASSES):
                queries = slice(o * NQ + h * P, o * NQ + (h + 1) * P)
                lo = o * span + e * PAGE
                q_lo = o * span + N + h * P
                nc.tensor.matmul_mx(
                    out=acc[:],
                    lhsT=qw[:, queries].bitcast(FP8X4),
                    lhsT_scale=planes[:, q_lo : q_lo + P],
                    rhs=words[e][:, o, :].bitcast(FP4X4),
                    rhs_scale=planes[:, lo : lo + PAGE],
                    start=(o == 0),
                    stop=(o == PASSES - 1),
                )
            nc.vector.tensor_tensor(
                out=scores[h][:, e * PAGE : (e + 1) * PAGE], in0=acc[:], in1=bias[e][:], op=ALU.add
            )

        for e in range(PAGES):
            for h in range(HALVES):
                score(h, e)
        for h in range(HALVES):
            nc.vector.tensor_reduce(out=neg_max[h][:], in_=scores[h][:], axis=AXIS.X, op=ALU.max, negate=True)

        vw = placed("vw", [P, PAGES * DV], U32, bias_at + 4 * PAGE * bias_place[2])
        nc.vector.tensor_copy(vw[:], vw_pool[:].indirect(voffsets[:]))

        page_sum = [sbuf("page_sum%d" % h, [P, PAGES], F32) for h in range(HALVES)]
        sums = [None] * HALVES

        def weigh(h, e):
            probs = sbuf("probs%d_%d" % (h, e), [P, PACK, P], F32)
            nc.scalar.activation(
                out=probs[:].rearrange("q r s -> q s r"),
                in_=scores[h][:, e * PAGE : (e + 1) * PAGE].rearrange("q (s r) -> q s r", r=PACK),
                func=ACT.Exp,
                bias=neg_max[h][:],
                accum_out=page_sum[h][:, e : e + 1],
            )
            turned = bank(TURN_BANK[h][e], "probs_turned%d_%d" % (h, e))
            for r in range(PACK):
                nc.tensor.transpose(turned[:, r * P : (r + 1) * P], probs[:, r, :], ident[:])
            weights = sbuf("weights%d_%d" % (h, e), [P, P, PACK], BF16)
            nc.vector.tensor_tensor(
                out=weights[:],
                in0=turned[:].rearrange("s (r q) -> s q r", r=PACK),
                in1=vs_cols[e][:].unsqueeze(1).to_broadcast([P, P, PACK]),
                op=ALU.mult,
            )
            return weights

        def quantise(h, e, weights):
            codes = sbuf("w_codes%d_%d" % (h, e), [P, P], U32)
            plane = sbuf("w_plane%d_%d" % (h, e), [P, P], U8)
            nc.vector.quantize_mx(
                out=codes[:].bitcast(FP8X4), scales=plane[:], in_=weights[:].rearrange("s q r -> s (q r)")
            )
            return codes, plane

        def multiply(h, e, codes, plane):
            nc.tensor.matmul_mx(
                out=sums[h][:, 0:DV],
                lhsT=codes[:].bitcast(FP8X4),
                lhsT_scale=plane[:],
                rhs=vw[:, e * DV : (e + 1) * DV].bitcast(FP8X4),
                rhs_scale=vsc[:, e * DV : (e + 1) * DV],
                start=(e == 0),
                stop=(e == PAGES - 1),
            )

        def finish(h):
            total = sbuf("total%d" % h, [P, 1], F32)
            copied = sbuf("copied%d" % h, [P, PAGES], F32)
            nc.scalar.activation(out=copied[:], in_=page_sum[h][:], func=ACT.Identity, accum_out=total[:])
            inverse = sbuf("inverse%d" % h, [P, 1], F32)
            nc.vector.reciprocal(inverse[:], total[:])
            result = sbuf("result%d" % h, [P, DV], F32)
            nc.scalar.activation(out=result[:], in_=sums[h][:, 0:DV], func=ACT.Copy, scale=inverse[:])
            nc.sync.dma_start(out[0, h * P : (h + 1) * P, :], result[:])

        steps = [(h, e) for h in range(HALVES) for e in range(PAGES)]
        quantised = {}
        pending = None
        for h, e in steps:
            weights = weigh(h, e)
            if pending is not None:
                quantised[pending[:2]] = quantise(*pending)
            pending = (h, e, weights)
        quantised[pending[:2]] = quantise(*pending)
        for h in range(HALVES):
            sums[h] = bank(SUM_BANK[h], "sums%d" % h)
            for e in range(PAGES):
                multiply(h, e, *quantised[(h, e)])
            finish(h)
